import numpy as np
import ml_dtypes


def mxq(x, axis, fmt="e4m3"):
    dtype, down = {"e4m3": (ml_dtypes.float8_e4m3fn, 7), "e5m2": (ml_dtypes.float8_e5m2, 14)}[fmt]
    v = np.moveaxis(np.asarray(x, np.float32).astype(ml_dtypes.bfloat16).astype(np.float64), axis, -1)
    blocks = v.reshape(v.shape[:-1] + (-1, 32))
    amax = np.abs(blocks).max(-1, keepdims=True)
    byte = np.maximum(np.where(amax > 0, np.frexp(amax)[1] - 1 + 127, 0) - down, 1)
    scale = np.exp2(byte - 127.0)
    codes = (blocks / scale).astype(np.float32).astype(dtype).astype(np.float64)
    return np.moveaxis((codes * scale).reshape(v.shape), -1, axis)


WIDE = False


def mx_kscale(k):
    if not WIDE:
        return np.ones(k)
    levels = np.array([10, -10, 5, -5, 0])
    if k % 512:
        return np.exp2(np.random.permutation(np.resize(levels, k // 32))).repeat(32)
    a = np.empty((k // 512, 16))
    for p in range(k // 512):
        a[p, :8] = np.random.permutation(np.resize(levels, 8))
        for g in range(8):
            far = levels[np.abs(levels - a[p, g]) >= 10]
            a[p, g + 8] = far[np.random.randint(len(far))]
    return np.exp2(a.ravel()).repeat(32)


BF16 = ml_dtypes.bfloat16


def bf(x):
    return np.asarray(x, np.float32).astype(BF16)


def f64(x):
    return np.asarray(x).astype(np.float64)

def planes(Y):
    n, m = Y.shape
    b = f64(bf(Y)).reshape(n // 32, 32, m)
    amax = np.abs(b).max(1)
    byte = np.clip(np.where(amax > 0, np.frexp(amax)[1] - 1 + 127 - 7, 1), 1, 254)
    codes = (b * np.exp2(127.0 - byte)[:, None, :]).reshape(n, m).astype(np.float32).astype(ml_dtypes.float8_e4m3fn).view(np.uint8)
    words = codes.reshape(n // 512, 128, 4, m).transpose(0, 1, 3, 2)
    return np.ascontiguousarray(words), np.ascontiguousarray(byte.astype(np.uint8).reshape(n // 512, 16, m))


N, M, P = 1024, 1024, 512


def dress_left(t, g, b):
    y = mxq(t, 1, "e4m3") @ mxq(g[:, None] * b, 0, "e4m3")
    return b + y


def dress_right(t, g, b):
    y = mxq(t, 0, "e4m3").T @ mxq(g[:, None] * b, 0, "e4m3")
    return b + y


def setup_inputs():
    s, u, t = mx_kscale(N), mx_kscale(M), mx_kscale(P)
    return {
        "ta": bf(np.random.standard_normal((N, N)) / np.sqrt(N) / s[None, :]),
        "tb": bf(np.random.standard_normal((M, M)) / np.sqrt(M) / u[:, None]),
        "ba": bf(np.random.standard_normal((N, P)) * P ** -0.25 * t[None, :]),
        "bb": bf(np.random.standard_normal((M, P)) * P ** -0.25 / t[None, :]),
        "ga": bf((1.0 + 0.1 * np.random.standard_normal(N)) * s),
        "gb": bf((1.0 + 0.1 * np.random.standard_normal(M)) * u),
        "delta": bf(np.random.uniform(0.5, 1.5, (N, M))),
    }


def core(ta, tb, ba, bb, ga, gb, delta):
    xa = dress_left(f64(ta), f64(ga), f64(ba))
    xb = dress_right(f64(tb), f64(gb), f64(bb))
    r = mxq(xa, 1, "e4m3") @ mxq(xb, 1, "e4m3").T
    tab = -r / f64(delta)
    return tab


def reference(ta, tb, ba, bb, ga, gb, delta):
    R_out = core(ta, tb, ba, bb, ga, gb, delta)
    words, scales = planes(R_out.T)
    return R_out, words, scales

@@ -1,0 +1,364 @@
+from contextlib import ExitStack
+
+import concourse.mybir as mybir
+from concourse.masks import make_identity
+
+F32 = mybir.dt.float32
+BF16 = mybir.dt.bfloat16
+I32 = mybir.dt.int32
+U32 = mybir.dt.uint32
+U8 = mybir.dt.uint8
+FP8X4 = mybir.dt.float8_e4m3fn_x4
+ALU = mybir.AluOpType
+ACT = mybir.ActivationFunctionType
+
+N, M, P = 1024, 1024, 512
+FLOPS = 2 * N * N * P + 2 * M * M * P + 2 * N * M * P
+BLOCKS = N // 128
+
+
+def tile_opposedspindirectringamplitudeupdate_x1_kernel(tc, ta, tb, ba, bb, ga, gb, delta, out_0, out_1, out_2):
+    nc = tc.nc
+    with ExitStack() as ctx:
+        keep = ctx.enter_context(tc.tile_pool(name="keep", bufs=1))
+        pool = ctx.enter_context(tc.tile_pool(name="work", bufs=2))
+        psum = ctx.enter_context(tc.psum_pool(name="psum", bufs=2))
+
+        ident = keep.tile([128, 128], F32, name="ident", align_bytes=64)
+
+        def keep_tile(shape, dtype, name):
+            return keep.tile(shape, dtype, name=name, align_bytes=64)
+
+        graw = {}
+        for s in ("a", "b"):
+            graw[s] = keep_tile([128, 2, 4], BF16, "g" + s)
+        raw = {}
+        for s in ("a", "b"):
+            for c in range(2):
+                raw[s, c] = keep_tile([128, 4, P], BF16, "raw%s%d" % (s, c))
+        tbr = [pool.tile([128, 4, M], BF16, name="tbr%d" % c, tag="big", bufs=4, align_bytes=64) for c in range(2)]
+        tar = [keep_tile([128, 2, N], BF16, "tar%d" % i) for i in range(4)]
+        dr = [keep_tile([128, M], BF16, "dr%d" % b) for b in range(8)]
+        btr = {s: keep_tile([128, 1024, 4], BF16, "btr" + s) for s in ("a", "b")}
+        gcodes = {}
+        gscale = {}
+        for s in ("a", "b"):
+            for c in range(2):
+                gcodes[s, c] = keep_tile([128, 512], U32, "gcodes%s%d" % (s, c))
+                gscale[s, c] = keep_tile([128, 512], U8, "gscale%s%d" % (s, c))
+        tbcodes = [keep_tile([128, M], U32, "tbcodes%d" % c) for c in range(2)]
+        tbscale = [keep_tile([128, M], U8, "tbscale%d" % c) for c in range(2)]
+        xbcodes = keep_tile([128, M], U32, "xbcodes")
+        xbscale = keep_tile([128, M], U8, "xbscale")
+        pcodes = keep_tile([128, 2, N], U32, "pcodes")
+        pscale = keep_tile([128, 2, N], U8, "pscale")
+
+        make_identity(nc, ident[:])
+        with tc.manual_schedule():
+            nc.scalar.dma_start(out=graw["b"][:], in_=gb.rearrange("(c p j) -> p c j", p=128, j=4))
+            nc.scalar.dma_start(out=graw["a"][:], in_=ga.rearrange("(c p j) -> p c j", p=128, j=4))
+            for c in range(2):
+                nc.sync.dma_start(out=raw["b", c][:], in_=bb[512 * c : 512 * (c + 1), :].rearrange("(p j) w -> p j w", j=4))
+            for c in range(2):
+                nc.sync.dma_start(out=tbr[c][:], in_=tb[512 * c : 512 * (c + 1), :].rearrange("(p j) w -> p j w", j=4))
+            for c in range(2):
+                nc.sync.dma_start(out=raw["a", c][:], in_=ba[512 * c : 512 * (c + 1), :].rearrange("(p j) w -> p j w", j=4))
+            for i in range(4):
+                nc.sync.dma_start(out=tar[i][:], in_=ta[256 * i : 256 * (i + 1), :].rearrange("(b p) k -> p b k", p=128))
+                nc.sync.dma_start(out=dr[i][:], in_=delta[128 * i : 128 * (i + 1), :])
+            for b in range(4, 8):
+                nc.sync.dma_start(out=dr[b][:], in_=delta[128 * b : 128 * (b + 1), :])
+
+            def factor(s, c):
+                gi = pool.tile([128, 4, 128, 4], BF16, name="gi", align_bytes=64)
+                nc.vector.tensor_tensor(
+                    out=gi[:],
+                    in0=raw[s, c][:].rearrange("p j (m t) -> p t m j", t=4),
+                    in1=graw[s][:, c, :].unsqueeze(1).unsqueeze(1).to_broadcast([128, 4, 128, 4]),
+                    op=ALU.mult,
+                )
+                return gi
+
+            def factor_quantise(s, c, gi):
+                nc.vector.quantize_mx(
+                    out=gcodes[s, c][:].bitcast(FP8X4), scales=gscale[s, c][:], in_=gi[:].rearrange("p t m j -> p (t m j)")
+                )
+
+            def turn_b(s, c, h):
+                words = raw[s, c][:].rearrange("p j w -> p (j w)").bitcast(F32)
+                bank = psum.tile([128, 4, 128], F32, name="turn", bufs=3)
+                for jj in range(2):
+                    for u in range(2):
+                        j = 2 * h + jj
+                        nc.tensor.transpose(bank[:, 2 * jj + u, :], words[:, 256 * j + u : 256 * (j + 1) : 2], ident[:])
+                dst = btr[s][:].rearrange("p n f -> p (n f)").bitcast(F32)
+                dst = dst[:, 1024 * c : 1024 * (c + 1)].rearrange("p (q r) -> p q r", r=8)[:, :, 4 * h : 4 * h + 4]
+                nc.scalar.copy(out=dst, in_=bank[:].rearrange("p r q -> p q r"))
+
+            def tb_copy(c, h, engine):
+                ti = pool.tile([128, 512, 4], BF16, name="ti", bufs=4, align_bytes=64)
+                src = tbr[c][:, :, 512 * h : 512 * (h + 1)].rearrange("p j w -> p w j")
+                if engine == "v":
+                    nc.vector.tensor_copy(out=ti[:], in_=src)
+                else:
+                    nc.scalar.copy(out=ti[:], in_=src)
+                return ti
+
+            def tb_quantise(c, h, ti):
+                cols = slice(512 * h, 512 * (h + 1))
+                nc.vector.quantize_mx(
+                    out=tbcodes[c][:, cols].bitcast(FP8X4), scales=tbscale[c][:, cols], in_=ti[:].rearrange("p w j -> p (w j)")
+                )
+
+            def turn_ta(b):
+                words = tar[b // 2][:, b % 2, :].bitcast(F32)
+                bank = psum.tile([128, 4, 128], F32, name="turn", bufs=3)
+                for c in range(2):
+                    for u in range(2):
+                        nc.tensor.transpose(bank[:, 2 * c + u, :], words[:, 256 * c + u : 256 * (c + 1) : 2], ident[:])
+                tat = pool.tile([128, 2, 128, 4], BF16, name="tat", bufs=8, align_bytes=64)
+                nc.scalar.copy(
+                    out=tat[:].rearrange("p c n f -> p (c n f)").bitcast(F32).rearrange("p (c n u) -> p c n u", c=2, u=2),
+                    in_=bank[:].rearrange("p (c u) n -> p c n u", c=2),
+                )
+                return tat
+
+            def ta_quantise(tat):
+                codes = pool.tile([128, 2, 128], U32, name="tacodes", bufs=8, align_bytes=64)
+                scale = pool.tile([128, 2, 128], U8, name="tascale", bufs=8, align_bytes=64)
+                nc.vector.quantize_mx(
+                    out=codes[:].rearrange("p c n -> p (c n)").bitcast(FP8X4),
+                    scales=scale[:].rearrange("p c n -> p (c n)"),
+                    in_=tat[:].rearrange("p c n f -> p (c n f)"),
+                )
+                return codes, scale
+
+            def dress_mm(s, moving):
+                bank = psum.tile([128, 4, 128], F32, name="dress", bufs=2)
+                for t in range(4):
+                    cols = slice(128 * t, 128 * (t + 1))
+                    for c in range(2):
+                        codes, scale = moving(c)
+                        nc.tensor.matmul_mx(
+                            out=bank[:, t, :],
+                            lhsT=gcodes[s, c][:, cols].bitcast(FP8X4),
+                            lhsT_scale=gscale[s, c][:, cols],
+                            rhs=codes.bitcast(FP8X4),
+                            rhs_scale=scale,
+                            start=(c == 0),
+                            stop=(c == 1),
+                        )
+                return bank
+
+            def dress_add(s, b, bank, out):
+                nc.vector.tensor_tensor(
+                    out=out, in0=bank[:].rearrange("p t n -> p n t"), in1=btr[s][:, 128 * b : 128 * (b + 1), :], op=ALU.add
+                )
+
+            def xb_mm(b):
+                cols = slice(128 * b, 128 * (b + 1))
+                return dress_mm("b", lambda c: (tbcodes[c][:, cols], tbscale[c][:, cols]))
+
+            def xa_mm(b, tacs):
+                return dress_mm("a", lambda c: (tacs[0][:, c, :], tacs[1][:, c, :]))
+
+            recs = {}
+
+            def root(b):
+                if b % 2 == 0:
+                    recs[b // 2] = pool.tile([128, 2, M], F32, name="recs", tag="big", bufs=4, align_bytes=64)
+                nc.scalar.activation(out=recs[b // 2][:, b % 2, :], in_=dr[b][:], func=ACT.Abs_reciprocal_sqrt)
+
+            def square(b):
+                rec = recs[b // 2][:, b % 2, :]
+                nc.scalar.activation(out=rec, in_=rec, func=ACT.Square)
+
+            gi = [factor("b", c) for c in range(2)]
+            for c in range(2):
+                for h in range(2):
+                    turn_b("b", c, h)
+            ti = {}
+            factor_quantise("b", 0, gi[0])
+            ti[0, 0] = tb_copy(0, 0, "v")
+            ti[0, 1] = tb_copy(0, 1, "s")
+            factor_quantise("b", 1, gi[1])
+            tb_quantise(0, 0, ti[0, 0])
+            ti[1, 0] = tb_copy(1, 0, "s")
+            ti[1, 1] = tb_copy(1, 1, "s")
+            gi = [factor("a", 0)]
+            tb_quantise(0, 1, ti[0, 1])
+            tb_quantise(1, 0, ti[1, 0])
+            turn_b("a", 0, 0)
+            turn_b("a", 0, 1)
+            root(0)
+            xbt = {}
+
+            def xb_pair(q):
+                xbt[q] = pool.tile([128, 256, 4], BF16, name="xbt", bufs=3, align_bytes=64)
+                for i in range(2):
+                    bank = xb_mm(2 * q + i)
+                    dress_add("b", 2 * q + i, bank, xbt[q][:, 128 * i : 128 * (i + 1), :])
+
+            def xb_quantise(q):
+                cols = slice(256 * q, 256 * (q + 1))
+                nc.vector.quantize_mx(
+                    out=xbcodes[:, cols].bitcast(FP8X4), scales=xbscale[:, cols], in_=xbt[q][:].rearrange("p n f -> p (n f)")
+                )
+
+            tat = {}
+            tac = {}
+            xb_pair(0)
+            turn_b("a", 1, 0)
+            turn_b("a", 1, 1)
+            root(1)
+            gi.append(factor("a", 1))
+            xb_pair(1)
+            tb_quantise(1, 1, ti[1, 1])
+            tat[0] = turn_ta(0)
+            tat[1] = turn_ta(1)
+            xb_quantise(0)
+            square(0)
+            tat[2] = turn_ta(2)
+            tat[3] = turn_ta(3)
+            factor_quantise("a", 0, gi[0])
+            xb_pair(2)
+            square(1)
+            factor_quantise("a", 1, gi[1])
+            xb_quantise(1)
+            tac[0] = ta_quantise(tat[0])
+            xb_pair(3)
+            tat[4] = turn_ta(4)
+            tat[5] = turn_ta(5)
+            root(2)
+            tac[1] = ta_quantise(tat[1])
+            xb_quantise(2)
+            tac[2] = ta_quantise(tat[2])
+            tat[6] = turn_ta(6)
+            tat[7] = turn_ta(7)
+            root(3)
+            square(2)
+            xb_quantise(3)
+            tac[3] = ta_quantise(tat[3])
+
+            xa = {}
+            xac = {}
+
+            xab = {}
+
+            def xa_add(b):
+                bank = xab[b]
+                xa[b] = pool.tile([128, 128, 4], BF16, name="xa", bufs=3, align_bytes=64)
+                dress_add("a", b, bank, xa[b][:])
+
+            def xa_quantise(b):
+                codes = pool.tile([128, 128], U32, name="xacodes", bufs=3, align_bytes=64)
+                scale = pool.tile([128, 128], U8, name="xascale", bufs=3, align_bytes=64)
+                nc.vector.quantize_mx(out=codes[:].bitcast(FP8X4), scales=scale[:], in_=xa[b][:].rearrange("p n f -> p (n f)"))
+                xac[b] = codes, scale
+
+            r = {}
+            rb = {}
+
+            def product(b, h):
+                cols = slice(512 * h, 512 * (h + 1))
+                bank = psum.tile([128, 512], F32, name="prod", bufs=3)
+                nc.tensor.matmul_mx(
+                    out=bank[:],
+                    lhsT=xac[b][0][:].bitcast(FP8X4),
+                    lhsT_scale=xac[b][1][:],
+                    rhs=xbcodes[:, cols].bitcast(FP8X4),
+                    rhs_scale=xbscale[:, cols],
+                    start=True,
+                    stop=True,
+                )
+                return bank
+
+            def divide(b, h, bank):
+                cols = slice(512 * h, 512 * (h + 1))
+                if h == 0:
+                    r[b] = pool.tile([128, M], F32, name="r", bufs=4)
+                    rb[b] = pool.tile([128, M], BF16, name="rb", bufs=3)
+                nc.vector.scalar_tensor_tensor(
+                    out=r[b][:, cols], in0=bank[:], scalar=-1.0, in1=recs[b // 2][:, b % 2, cols], op0=ALU.mult, op1=ALU.mult
+                )
+                if b == BLOCKS - 1:
+                    nc.vector.tensor_copy(out=rb[b][:, cols], in_=r[b][:, cols])
+                else:
+                    nc.gpsimd.tensor_scalar(
+                        out=rb[b][:, cols], in0=r[b][:, cols], scalar1=1.0, scalar2=-0.0, op0=ALU.mult, op1=ALU.add
+                    )
+
+            pt = {}
+
+            def turn_p(b):
+                words = rb[b][:].bitcast(F32)
+                bank = psum.tile([128, 4, 128], F32, name="turn", bufs=3)
+                for g in range(2):
+                    for u in range(2):
+                        nc.tensor.transpose(bank[:, 2 * g + u, :], words[:, 256 * g + u : 256 * (g + 1) : 2], ident[:])
+                pt[b] = pool.tile([128, 2, 128, 4], BF16, name="pt", bufs=3, align_bytes=64)
+                nc.scalar.copy(
+                    out=pt[b][:].rearrange("p c n f -> p (c n f)").bitcast(F32).rearrange("p (c n u) -> p c n u", c=2, u=2),
+                    in_=bank[:].rearrange("p (c u) n -> p c n u", c=2),
+                )
+
+            def p_quantise(b, g):
+                cols = slice(128 * b, 128 * (b + 1))
+                nc.vector.quantize_mx(
+                    out=pcodes[:, g, cols].bitcast(FP8X4), scales=pscale[:, g, cols], in_=pt[b][:, g, :, :].rearrange("p n f -> p (n f)")
+                )
+
+            def store_r(b):
+                nc.sync.dma_start(out=out_0[128 * b : 128 * (b + 1), :], in_=r[b][:])
+
+            def store_p(b0, b1):
+                cols = slice(128 * b0, 128 * b1)
+                nc.sync.dma_start(
+                    out=out_1[:, :, cols, :].rearrange("g p n f -> p g (n f)").bitcast(I32), in_=pcodes[:, :, cols].bitcast(I32)
+                )
+                for q in range(4):
+                    nc.sync.dma_start(
+                        out=out_2[:, 4 * q : 4 * q + 4, cols].rearrange("g r n -> r g n").bitcast(I32),
+                        in_=pscale[32 * q : 32 * q + 4, :, cols].bitcast(I32),
+                    )
+
+            xab[0] = xa_mm(0, tac[0])
+            xab[1] = xa_mm(1, tac[1])
+            xa_add(0)
+            xa_add(1)
+            xab[2] = xa_mm(2, tac[2])
+            xa_quantise(0)
+            banks = {}
+            for h in range(2):
+                banks[0, h] = product(0, h)
+            for i in range(BLOCKS + 2):
+                if i < BLOCKS:
+                    divide(i, 0, banks[i, 0])
+                if i + 1 < BLOCKS:
+                    xa_quantise(i + 1)
+                    banks[i + 1, 0] = product(i + 1, 0)
+                if i < BLOCKS:
+                    divide(i, 1, banks[i, 1])
+                    store_r(i)
+                if i + 1 < BLOCKS:
+                    banks[i + 1, 1] = product(i + 1, 1)
+                if 1 <= i <= BLOCKS:
+                    turn_p(i - 1)
+                if i + 3 < BLOCKS:
+                    xab[i + 3] = xa_mm(i + 3, tac[i + 3])
+                if i + 4 < BLOCKS:
+                    root(i + 4)
+                    square(i + 3)
+                elif i + 3 < BLOCKS:
+                    square(i + 3)
+                if i >= 2:
+                    p_quantise(i - 2, 0)
+                if i + 4 < BLOCKS:
+                    tac[i + 4] = ta_quantise(tat[i + 4])
+                if i + 2 < BLOCKS:
+                    xa_add(i + 2)
+                if i >= 2:
+                    p_quantise(i - 2, 1)
+                if i == 5:
+                    store_p(0, 4)
+            store_p(4, 8)

@@ -30,8 +30,11 @@ def tile_opposedspindirectringamplitudeupdate_x1_kernel(tc, ta, tb, ba, bb, ga, 
             return keep.tile(shape, dtype, name=name, align_bytes=64)
 
         graw = {}
+        gf = {}
         for s in ("a", "b"):
             graw[s] = keep_tile([128, 2, 4], BF16, "g" + s)
+            gf[s] = keep_tile([128, 2, 4], F32, "gf" + s)
+        warm = keep.tile([128, 1], F32, name="warm")
         raw = {}
         for s in ("a", "b"):
             for c in range(2):
@@ -69,14 +72,18 @@ def tile_opposedspindirectringamplitudeupdate_x1_kernel(tc, ta, tb, ba, bb, ga, 
             for b in range(4, 8):
                 nc.sync.dma_start(out=dr[b][:], in_=delta[128 * b : 128 * (b + 1), :])
 
-            def factor(s, c):
+            gm = {}
+
+            def factor_mult(s, c):
+                gm[s, c] = pool.tile([128, 4, P], BF16, name="gm", align_bytes=64)
+                for j in range(4):
+                    nc.vector.tensor_scalar(
+                        out=gm[s, c][:, j, :], in0=raw[s, c][:, j, :], scalar1=gf[s][:, c, j : j + 1], scalar2=None, op0=ALU.mult
+                    )
+
+            def factor_copy(s, c):
                 gi = pool.tile([128, 4, 128, 4], BF16, name="gi", align_bytes=64)
-                nc.vector.tensor_tensor(
-                    out=gi[:],
-                    in0=raw[s, c][:].rearrange("p j (m t) -> p t m j", t=4),
-                    in1=graw[s][:, c, :].unsqueeze(1).unsqueeze(1).to_broadcast([128, 4, 128, 4]),
-                    op=ALU.mult,
-                )
+                nc.vector.tensor_copy(out=gi[:], in_=gm[s, c][:].rearrange("p j (m t) -> p t m j", t=4))
                 return gi
 
             def factor_quantise(s, c, gi):
@@ -134,7 +141,7 @@ def tile_opposedspindirectringamplitudeupdate_x1_kernel(tc, ta, tb, ba, bb, ga, 
                 return codes, scale
 
             def dress_mm(s, moving):
-                bank = psum.tile([128, 4, 128], F32, name="dress", bufs=2)
+                bank = psum.tile([128, 4, 128], F32, name="dress", tag="mm", bufs=5)
                 for t in range(4):
                     cols = slice(128 * t, 128 * (t + 1))
                     for c in range(2):
@@ -173,7 +180,14 @@ def tile_opposedspindirectringamplitudeupdate_x1_kernel(tc, ta, tb, ba, bb, ga, 
                 rec = recs[b // 2][:, b % 2, :]
                 nc.scalar.activation(out=rec, in_=rec, func=ACT.Square)
 
-            gi = [factor("b", c) for c in range(2)]
+            nc.vector.memset(warm[:], 1.0)
+            nc.scalar.activation(out=warm[:], in_=warm[:], func=ACT.Abs_reciprocal_sqrt)
+            for s in ("b", "a"):
+                nc.vector.tensor_copy(out=gf[s][:], in_=graw[s][:])
+            factor_mult("b", 0)
+            gi = [factor_copy("b", 0)]
+            factor_mult("b", 1)
+            gi.append(factor_copy("b", 1))
             for c in range(2):
                 for h in range(2):
                     turn_b("b", c, h)
@@ -185,19 +199,20 @@ def tile_opposedspindirectringamplitudeupdate_x1_kernel(tc, ta, tb, ba, bb, ga, 
             tb_quantise(0, 0, ti[0, 0])
             ti[1, 0] = tb_copy(1, 0, "s")
             ti[1, 1] = tb_copy(1, 1, "s")
-            gi = [factor("a", 0)]
+            factor_mult("a", 0)
             tb_quantise(0, 1, ti[0, 1])
             tb_quantise(1, 0, ti[1, 0])
+            gi = [factor_copy("a", 0)]
             turn_b("a", 0, 0)
             turn_b("a", 0, 1)
             root(0)
             xbt = {}
+            xbb = {}
 
-            def xb_pair(q):
-                xbt[q] = pool.tile([128, 256, 4], BF16, name="xbt", bufs=3, align_bytes=64)
-                for i in range(2):
-                    bank = xb_mm(2 * q + i)
-                    dress_add("b", 2 * q + i, bank, xbt[q][:, 128 * i : 128 * (i + 1), :])
+            def xb_add(b):
+                if b % 2 == 0:
+                    xbt[b // 2] = pool.tile([128, 256, 4], BF16, name="xbt", bufs=3, align_bytes=64)
+                dress_add("b", b, xbb[b], xbt[b // 2][:, 128 * (b % 2) : 128 * (b % 2) + 128, :])
 
             def xb_quantise(q):
                 cols = slice(256 * q, 256 * (q + 1))
@@ -207,43 +222,51 @@ def tile_opposedspindirectringamplitudeupdate_x1_kernel(tc, ta, tb, ba, bb, ga, 
 
             tat = {}
             tac = {}
-            xb_pair(0)
+            xab = {}
+            for b in range(4):
+                xbb[b] = xb_mm(b)
+            xb_add(0)
+            xb_add(1)
             turn_b("a", 1, 0)
+            factor_mult("a", 1)
             turn_b("a", 1, 1)
             root(1)
-            gi.append(factor("a", 1))
-            xb_pair(1)
-            tb_quantise(1, 1, ti[1, 1])
+            xb_add(2)
+            xb_add(3)
+            gi.append(factor_copy("a", 1))
             tat[0] = turn_ta(0)
             tat[1] = turn_ta(1)
+            tb_quantise(1, 1, ti[1, 1])
+            for b in range(4, 8):
+                xbb[b] = xb_mm(b)
             xb_quantise(0)
             square(0)
             tat[2] = turn_ta(2)
             tat[3] = turn_ta(3)
             factor_quantise("a", 0, gi[0])
-            xb_pair(2)
+            xb_add(4)
             square(1)
+            xb_add(5)
             factor_quantise("a", 1, gi[1])
             xb_quantise(1)
             tac[0] = ta_quantise(tat[0])
-            xb_pair(3)
+            xb_add(6)
             tat[4] = turn_ta(4)
             tat[5] = turn_ta(5)
             root(2)
             tac[1] = ta_quantise(tat[1])
+            xb_add(7)
             xb_quantise(2)
+            xab[0] = xa_mm(0, tac[0])
+            xab[1] = xa_mm(1, tac[1])
             tac[2] = ta_quantise(tat[2])
-            tat[6] = turn_ta(6)
-            tat[7] = turn_ta(7)
             root(3)
             square(2)
-            xb_quantise(3)
             tac[3] = ta_quantise(tat[3])
+            xb_quantise(3)
 
             xa = {}
             xac = {}
-
-            xab = {}
 
             def xa_add(b):
                 bank = xab[b]
@@ -261,7 +284,7 @@ def tile_opposedspindirectringamplitudeupdate_x1_kernel(tc, ta, tb, ba, bb, ga, 
 
             def product(b, h):
                 cols = slice(512 * h, 512 * (h + 1))
-                bank = psum.tile([128, 512], F32, name="prod", bufs=3)
+                bank = psum.tile([128, 512], F32, name="prod", tag="mm", bufs=5)
                 nc.tensor.matmul_mx(
                     out=bank[:],
                     lhsT=xac[b][0][:].bitcast(FP8X4),
@@ -281,12 +304,9 @@ def tile_opposedspindirectringamplitudeupdate_x1_kernel(tc, ta, tb, ba, bb, ga, 
                 nc.vector.scalar_tensor_tensor(
                     out=r[b][:, cols], in0=bank[:], scalar=-1.0, in1=recs[b // 2][:, b % 2, cols], op0=ALU.mult, op1=ALU.mult
                 )
-                if b == BLOCKS - 1:
-                    nc.vector.tensor_copy(out=rb[b][:, cols], in_=r[b][:, cols])
-                else:
-                    nc.gpsimd.tensor_scalar(
-                        out=rb[b][:, cols], in0=r[b][:, cols], scalar1=1.0, scalar2=-0.0, op0=ALU.mult, op1=ALU.add
-                    )
+
+            def narrow(b):
+                nc.vector.tensor_copy(out=rb[b][:], in_=r[b][:])
 
             pt = {}
 
@@ -322,8 +342,6 @@ def tile_opposedspindirectringamplitudeupdate_x1_kernel(tc, ta, tb, ba, bb, ga, 
                         in_=pscale[32 * q : 32 * q + 4, :, cols].bitcast(I32),
                     )
 
-            xab[0] = xa_mm(0, tac[0])
-            xab[1] = xa_mm(1, tac[1])
             xa_add(0)
             xa_add(1)
             xab[2] = xa_mm(2, tac[2])
@@ -342,6 +360,8 @@ def tile_opposedspindirectringamplitudeupdate_x1_kernel(tc, ta, tb, ba, bb, ga, 
                     store_r(i)
                 if i + 1 < BLOCKS:
                     banks[i + 1, 1] = product(i + 1, 1)
+                if i < 2:
+                    tat[i + 6] = turn_ta(i + 6)
                 if 1 <= i <= BLOCKS:
                     turn_p(i - 1)
                 if i + 3 < BLOCKS:
@@ -357,6 +377,8 @@ def tile_opposedspindirectringamplitudeupdate_x1_kernel(tc, ta, tb, ba, bb, ga, 
                     tac[i + 4] = ta_quantise(tat[i + 4])
                 if i + 2 < BLOCKS:
                     xa_add(i + 2)
+                if i < BLOCKS:
+                    narrow(i)
                 if i >= 2:
                     p_quantise(i - 2, 1)
                 if i == 5:

@@ -53,8 +53,8 @@ def tile_opposedspindirectringamplitudeupdate_x1_kernel(tc, ta, tb, ba, bb, ga, 
         tbscale = [keep_tile([128, M], U8, "tbscale%d" % c) for c in range(2)]
         xbcodes = keep_tile([128, M], U32, "xbcodes")
         xbscale = keep_tile([128, M], U8, "xbscale")
-        pcodes = keep_tile([128, 2, N], U32, "pcodes")
-        pscale = keep_tile([128, 2, N], U8, "pscale")
+        pcodes = [keep_tile([128, 2, 256], U32, "pcodes%d" % q) for q in range(4)]
+        pscale = keep_tile([128, 4, 2, 256], U8, "pscale")
 
         make_identity(nc, ident[:])
         with tc.manual_schedule():
@@ -91,6 +91,10 @@ def tile_opposedspindirectringamplitudeupdate_x1_kernel(tc, ta, tb, ba, bb, ga, 
                     out=gcodes[s, c][:].bitcast(FP8X4), scales=gscale[s, c][:], in_=gi[:].rearrange("p t m j -> p (t m j)")
                 )
 
+            tat = {}
+            tac = {}
+            xab = {}
+
             def turn_b(s, c, h):
                 words = raw[s, c][:].rearrange("p j w -> p (j w)").bitcast(F32)
                 bank = psum.tile([128, 4, 128], F32, name="turn", bufs=3)
@@ -104,11 +108,12 @@ def tile_opposedspindirectringamplitudeupdate_x1_kernel(tc, ta, tb, ba, bb, ga, 
 
             def tb_copy(c, h, engine):
                 ti = pool.tile([128, 512, 4], BF16, name="ti", bufs=4, align_bytes=64)
-                src = tbr[c][:, :, 512 * h : 512 * (h + 1)].rearrange("p j w -> p w j")
+                src = tbr[c][:, :, 512 * h : 512 * (h + 1)].rearrange("p j (w i) -> p w j i", i=4)
+                dst = ti[:].rearrange("p (w i) j -> p w j i", i=4)
                 if engine == "v":
-                    nc.vector.tensor_copy(out=ti[:], in_=src)
+                    nc.vector.tensor_copy(out=dst, in_=src)
                 else:
-                    nc.scalar.copy(out=ti[:], in_=src)
+                    nc.scalar.copy(out=dst, in_=src)
                 return ti
 
             def tb_quantise(c, h, ti):
@@ -123,22 +128,23 @@ def tile_opposedspindirectringamplitudeupdate_x1_kernel(tc, ta, tb, ba, bb, ga, 
                 for c in range(2):
                     for u in range(2):
                         nc.tensor.transpose(bank[:, 2 * c + u, :], words[:, 256 * c + u : 256 * (c + 1) : 2], ident[:])
-                tat = pool.tile([128, 2, 128, 4], BF16, name="tat", bufs=8, align_bytes=64)
+                half = slice(128 * (b % 2), 128 * (b % 2) + 128)
+                if b % 2 == 0:
+                    tat[b // 2] = pool.tile([128, 2, 256, 4], BF16, name="tat", bufs=4, align_bytes=64)
                 nc.scalar.copy(
-                    out=tat[:].rearrange("p c n f -> p (c n f)").bitcast(F32).rearrange("p (c n u) -> p c n u", c=2, u=2),
+                    out=tat[b // 2][:].rearrange("p c n f -> p (c n f)").bitcast(F32).rearrange("p (c n u) -> p c n u", c=2, u=2)[:, :, half, :],
                     in_=bank[:].rearrange("p (c u) n -> p c n u", c=2),
                 )
-                return tat
 
-            def ta_quantise(tat):
-                codes = pool.tile([128, 2, 128], U32, name="tacodes", bufs=8, align_bytes=64)
-                scale = pool.tile([128, 2, 128], U8, name="tascale", bufs=8, align_bytes=64)
+            def ta_quantise(q):
+                codes = pool.tile([128, 2, 256], U32, name="tacodes", bufs=4, align_bytes=64)
+                scale = pool.tile([128, 2, 256], U8, name="tascale", bufs=4, align_bytes=64)
                 nc.vector.quantize_mx(
                     out=codes[:].rearrange("p c n -> p (c n)").bitcast(FP8X4),
                     scales=scale[:].rearrange("p c n -> p (c n)"),
-                    in_=tat[:].rearrange("p c n f -> p (c n f)"),
+                    in_=tat[q][:].rearrange("p c n f -> p (c n f)"),
                 )
-                return codes, scale
+                tac[q] = codes, scale
 
             def dress_mm(s, moving):
                 bank = psum.tile([128, 4, 128], F32, name="dress", tag="mm", bufs=5)
@@ -166,8 +172,10 @@ def tile_opposedspindirectringamplitudeupdate_x1_kernel(tc, ta, tb, ba, bb, ga, 
                 cols = slice(128 * b, 128 * (b + 1))
                 return dress_mm("b", lambda c: (tbcodes[c][:, cols], tbscale[c][:, cols]))
 
-            def xa_mm(b, tacs):
-                return dress_mm("a", lambda c: (tacs[0][:, c, :], tacs[1][:, c, :]))
+            def xa_mm(b):
+                cols = slice(128 * (b % 2), 128 * (b % 2) + 128)
+                codes, scale = tac[b // 2]
+                xab[b] = dress_mm("a", lambda c: (codes[:, c, cols], scale[:, c, cols]))
 
             recs = {}
 
@@ -210,19 +218,16 @@ def tile_opposedspindirectringamplitudeupdate_x1_kernel(tc, ta, tb, ba, bb, ga, 
             xbb = {}
 
             def xb_add(b):
-                if b % 2 == 0:
-                    xbt[b // 2] = pool.tile([128, 256, 4], BF16, name="xbt", bufs=3, align_bytes=64)
-                dress_add("b", b, xbb[b], xbt[b // 2][:, 128 * (b % 2) : 128 * (b % 2) + 128, :])
+                if b % 4 == 0:
+                    xbt[b // 4] = pool.tile([128, 512, 4], BF16, name="xbt", bufs=2, align_bytes=64)
+                dress_add("b", b, xbb[b], xbt[b // 4][:, 128 * (b % 4) : 128 * (b % 4) + 128, :])
 
             def xb_quantise(q):
-                cols = slice(256 * q, 256 * (q + 1))
+                cols = slice(512 * q, 512 * (q + 1))
                 nc.vector.quantize_mx(
                     out=xbcodes[:, cols].bitcast(FP8X4), scales=xbscale[:, cols], in_=xbt[q][:].rearrange("p n f -> p (n f)")
                 )
 
-            tat = {}
-            tac = {}
-            xab = {}
             for b in range(4):
                 xbb[b] = xb_mm(b)
             xb_add(0)
@@ -234,36 +239,32 @@ def tile_opposedspindirectringamplitudeupdate_x1_kernel(tc, ta, tb, ba, bb, ga, 
             xb_add(2)
             xb_add(3)
             gi.append(factor_copy("a", 1))
-            tat[0] = turn_ta(0)
-            tat[1] = turn_ta(1)
+            turn_ta(0)
+            turn_ta(1)
             tb_quantise(1, 1, ti[1, 1])
             for b in range(4, 8):
                 xbb[b] = xb_mm(b)
             xb_quantise(0)
             square(0)
-            tat[2] = turn_ta(2)
-            tat[3] = turn_ta(3)
+            turn_ta(2)
+            turn_ta(3)
             factor_quantise("a", 0, gi[0])
             xb_add(4)
             square(1)
             xb_add(5)
             factor_quantise("a", 1, gi[1])
-            xb_quantise(1)
-            tac[0] = ta_quantise(tat[0])
+            ta_quantise(0)
             xb_add(6)
-            tat[4] = turn_ta(4)
-            tat[5] = turn_ta(5)
+            turn_ta(4)
+            turn_ta(5)
             root(2)
-            tac[1] = ta_quantise(tat[1])
             xb_add(7)
-            xb_quantise(2)
-            xab[0] = xa_mm(0, tac[0])
-            xab[1] = xa_mm(1, tac[1])
-            tac[2] = ta_quantise(tat[2])
+            xa_mm(0)
+            xa_mm(1)
             root(3)
             square(2)
-            tac[3] = ta_quantise(tat[3])
-            xb_quantise(3)
+            ta_quantise(1)
+            xb_quantise(1)
 
             xa = {}
             xac = {}
@@ -305,82 +306,112 @@ def tile_opposedspindirectringamplitudeupdate_x1_kernel(tc, ta, tb, ba, bb, ga, 
                     out=r[b][:, cols], in0=bank[:], scalar=-1.0, in1=recs[b // 2][:, b % 2, cols], op0=ALU.mult, op1=ALU.mult
                 )
 
-            def narrow(b):
-                nc.vector.tensor_copy(out=rb[b][:], in_=r[b][:])
+            def narrow(b, c0, c1):
+                nc.vector.tensor_copy(out=rb[b][:, c0:c1], in_=r[b][:, c0:c1])
 
             pt = {}
 
-            def turn_p(b):
+            pb = {}
+
+            def turn_p(b, g):
                 words = rb[b][:].bitcast(F32)
-                bank = psum.tile([128, 4, 128], F32, name="turn", bufs=3)
-                for g in range(2):
-                    for u in range(2):
-                        nc.tensor.transpose(bank[:, 2 * g + u, :], words[:, 256 * g + u : 256 * (g + 1) : 2], ident[:])
-                pt[b] = pool.tile([128, 2, 128, 4], BF16, name="pt", bufs=3, align_bytes=64)
+                if g == 0:
+                    pb[b] = psum.tile([128, 4, 128], F32, name="turn", bufs=3)
+                for u in range(2):
+                    nc.tensor.transpose(pb[b][:, 2 * g + u, :], words[:, 256 * g + u : 256 * (g + 1) : 2], ident[:])
+
+            def p_words(b, g0, g1):
+                half = slice(128 * (b % 2), 128 * (b % 2) + 128)
+                if b % 2 == 0 and g0 == 0:
+                    pt[b // 2] = pool.tile([128, 2, 256, 4], BF16, name="pt", bufs=2, align_bytes=64)
                 nc.scalar.copy(
-                    out=pt[b][:].rearrange("p c n f -> p (c n f)").bitcast(F32).rearrange("p (c n u) -> p c n u", c=2, u=2),
-                    in_=bank[:].rearrange("p (c u) n -> p c n u", c=2),
+                    out=pt[b // 2][:].rearrange("p c n f -> p (c n f)").bitcast(F32).rearrange("p (c n u) -> p c n u", c=2, u=2)[:, g0:g1, half, :],
+                    in_=pb[b][:, 2 * g0 : 2 * g1, :].rearrange("p (c u) n -> p c n u", u=2),
+                )
+
+            def p_quantise_pair(q):
+                nc.vector.quantize_mx(
+                    out=pcodes[q][:].rearrange("p g n -> p (g n)").bitcast(FP8X4),
+                    scales=pscale[:, q, :, :].rearrange("p g n -> p (g n)"),
+                    in_=pt[q][:].rearrange("p g n f -> p (g n f)"),
                 )
 
             def p_quantise(b, g):
-                cols = slice(128 * b, 128 * (b + 1))
+                half = slice(128 * (b % 2), 128 * (b % 2) + 128)
                 nc.vector.quantize_mx(
-                    out=pcodes[:, g, cols].bitcast(FP8X4), scales=pscale[:, g, cols], in_=pt[b][:, g, :, :].rearrange("p n f -> p (n f)")
+                    out=pcodes[b // 2][:, g, half].bitcast(FP8X4),
+                    scales=pscale[:, b // 2, g, half],
+                    in_=pt[b // 2][:, g, half, :].rearrange("p n f -> p (n f)"),
                 )
 
             def store_r(b):
                 nc.sync.dma_start(out=out_0[128 * b : 128 * (b + 1), :], in_=r[b][:])
 
-            def store_p(b0, b1):
-                cols = slice(128 * b0, 128 * b1)
+            def store_codes(b0, b1):
+                n = 128 * (b1 - b0)
+                n0 = 128 * (b0 % 2)
                 nc.sync.dma_start(
-                    out=out_1[:, :, cols, :].rearrange("g p n f -> p g (n f)").bitcast(I32), in_=pcodes[:, :, cols].bitcast(I32)
+                    out=out_1[:, :, 128 * b0 : 128 * b1, :].rearrange("g p n f -> p g (n f)").bitcast(I32),
+                    in_=pcodes[b0 // 2][:, :, n0 : n0 + n].bitcast(I32),
                 )
-                for q in range(4):
-                    nc.sync.dma_start(
-                        out=out_2[:, 4 * q : 4 * q + 4, cols].rearrange("g r n -> r g n").bitcast(I32),
-                        in_=pscale[32 * q : 32 * q + 4, :, cols].bitcast(I32),
+
+            def store_scales(q, queues):
+                for quad in range(4):
+                    queues[quad % 2].dma_start(
+                        out=out_2[:, 4 * quad : 4 * quad + 4, 256 * q : 256 * (q + 1)].rearrange("g r n -> r g n").bitcast(I32),
+                        in_=pscale[32 * quad : 32 * quad + 4, q, :, :].bitcast(I32),
                     )
 
             xa_add(0)
             xa_add(1)
-            xab[2] = xa_mm(2, tac[2])
+            xa_mm(2)
             xa_quantise(0)
             banks = {}
             for h in range(2):
                 banks[0, h] = product(0, h)
-            for i in range(BLOCKS + 2):
-                if i < BLOCKS:
-                    divide(i, 0, banks[i, 0])
+            last = BLOCKS - 1
+            for i in range(BLOCKS):
+                divide(i, 0, banks[i, 0])
+                if i >= 3 and i % 2 == 1:
+                    p_quantise_pair(i // 2 - 1)
+                    store_codes(i - 3, i - 1)
+                    store_scales(i // 2 - 1, (nc.sync, nc.sync))
                 if i + 1 < BLOCKS:
                     xa_quantise(i + 1)
                     banks[i + 1, 0] = product(i + 1, 0)
-                if i < BLOCKS:
-                    divide(i, 1, banks[i, 1])
-                    store_r(i)
+                else:
+                    narrow(i, 0, 512)
+                divide(i, 1, banks[i, 1])
+                store_r(i)
                 if i + 1 < BLOCKS:
                     banks[i + 1, 1] = product(i + 1, 1)
                 if i < 2:
-                    tat[i + 6] = turn_ta(i + 6)
-                if 1 <= i <= BLOCKS:
-                    turn_p(i - 1)
+                    turn_ta(i + 6)
+                if i >= 1:
+                    turn_p(i - 1, 0)
+                    turn_p(i - 1, 1)
+                    p_words(i - 1, 0, 2)
                 if i + 3 < BLOCKS:
-                    xab[i + 3] = xa_mm(i + 3, tac[i + 3])
+                    xa_mm(i + 3)
                 if i + 4 < BLOCKS:
                     root(i + 4)
+                if i + 3 < BLOCKS:
                     square(i + 3)
-                elif i + 3 < BLOCKS:
-                    square(i + 3)
-                if i >= 2:
-                    p_quantise(i - 2, 0)
-                if i + 4 < BLOCKS:
-                    tac[i + 4] = ta_quantise(tat[i + 4])
+                if i in (0, 2):
+                    ta_quantise(2 + i // 2)
                 if i + 2 < BLOCKS:
                     xa_add(i + 2)
-                if i < BLOCKS:
-                    narrow(i)
-                if i >= 2:
-                    p_quantise(i - 2, 1)
-                if i == 5:
-                    store_p(0, 4)
-            store_p(4, 8)
+                if i < last:
+                    narrow(i, 0, M)
+            turn_p(last, 0)
+            p_words(last, 0, 1)
+            narrow(last, 512, M)
+            p_quantise(last - 1, 0)
+            p_quantise(last - 1, 1)
+            store_codes(last - 1, last)
+            turn_p(last, 1)
+            p_words(last, 1, 2)
+            p_quantise(last, 0)
+            p_quantise(last, 1)
+            store_codes(last, BLOCKS)
+            store_scales(3, (nc.sync, nc.scalar))

@@ -147,7 +147,7 @@ def tile_opposedspindirectringamplitudeupdate_x1_kernel(tc, ta, tb, ba, bb, ga, 
                 tac[q] = codes, scale
 
             def dress_mm(s, moving):
-                bank = psum.tile([128, 4, 128], F32, name="dress", tag="mm", bufs=5)
+                bank = psum.tile([128, 4, 128], F32, name="dress", tag="mm", bufs=4)
                 for t in range(4):
                     cols = slice(128 * t, 128 * (t + 1))
                     for c in range(2):
@@ -167,6 +167,20 @@ def tile_opposedspindirectringamplitudeupdate_x1_kernel(tc, ta, tb, ba, bb, ga, 
                 nc.vector.tensor_tensor(
                     out=out, in0=bank[:].rearrange("p t n -> p n t"), in1=btr[s][:, 128 * b : 128 * (b + 1), :], op=ALU.add
                 )
+
+            spare = psum.tile([128, 512], F32, name="spare", bufs=1)
+
+            def busy(n):
+                for i in range(n):
+                    nc.tensor.matmul_mx(
+                        out=spare[:],
+                        lhsT=gcodes["b", 0][:, 0:128].bitcast(FP8X4),
+                        lhsT_scale=gscale["b", 0][:, 0:128],
+                        rhs=gcodes["b", 0][:].bitcast(FP8X4),
+                        rhs_scale=gscale["b", 0][:],
+                        start=True,
+                        stop=True,
+                    )
 
             def xb_mm(b):
                 cols = slice(128 * b, 128 * (b + 1))
@@ -203,6 +217,7 @@ def tile_opposedspindirectringamplitudeupdate_x1_kernel(tc, ta, tb, ba, bb, ga, 
             factor_quantise("b", 0, gi[0])
             ti[0, 0] = tb_copy(0, 0, "v")
             ti[0, 1] = tb_copy(0, 1, "s")
+            busy(4)
             factor_quantise("b", 1, gi[1])
             tb_quantise(0, 0, ti[0, 0])
             ti[1, 0] = tb_copy(1, 0, "s")
@@ -213,6 +228,7 @@ def tile_opposedspindirectringamplitudeupdate_x1_kernel(tc, ta, tb, ba, bb, ga, 
             gi = [factor_copy("a", 0)]
             turn_b("a", 0, 0)
             turn_b("a", 0, 1)
+            busy(2)
             root(0)
             xbt = {}
             xbb = {}
@@ -241,6 +257,7 @@ def tile_opposedspindirectringamplitudeupdate_x1_kernel(tc, ta, tb, ba, bb, ga, 
             gi.append(factor_copy("a", 1))
             turn_ta(0)
             turn_ta(1)
+            busy(1)
             tb_quantise(1, 1, ti[1, 1])
             for b in range(4, 8):
                 xbb[b] = xb_mm(b)
@@ -248,6 +265,7 @@ def tile_opposedspindirectringamplitudeupdate_x1_kernel(tc, ta, tb, ba, bb, ga, 
             square(0)
             turn_ta(2)
             turn_ta(3)
+            busy(1)
             factor_quantise("a", 0, gi[0])
             xb_add(4)
             square(1)
@@ -257,6 +275,7 @@ def tile_opposedspindirectringamplitudeupdate_x1_kernel(tc, ta, tb, ba, bb, ga, 
             xb_add(6)
             turn_ta(4)
             turn_ta(5)
+            busy(1)
             root(2)
             xb_add(7)
             xa_mm(0)
@@ -285,7 +304,7 @@ def tile_opposedspindirectringamplitudeupdate_x1_kernel(tc, ta, tb, ba, bb, ga, 
 
             def product(b, h):
                 cols = slice(512 * h, 512 * (h + 1))
-                bank = psum.tile([128, 512], F32, name="prod", tag="mm", bufs=5)
+                bank = psum.tile([128, 512], F32, name="prod", tag="mm", bufs=4)
                 nc.tensor.matmul_mx(
                     out=bank[:],
                     lhsT=xac[b][0][:].bitcast(FP8X4),
@@ -306,8 +325,12 @@ def tile_opposedspindirectringamplitudeupdate_x1_kernel(tc, ta, tb, ba, bb, ga, 
                     out=r[b][:, cols], in0=bank[:], scalar=-1.0, in1=recs[b // 2][:, b % 2, cols], op0=ALU.mult, op1=ALU.mult
                 )
 
-            def narrow(b, c0, c1):
-                nc.vector.tensor_copy(out=rb[b][:, c0:c1], in_=r[b][:, c0:c1])
+            def narrow(b, g0, g1):
+                pairs = slice(128 * g0, 128 * g1)
+                nc.vector.tensor_copy(
+                    out=rb[b][:].rearrange("p (u w e) -> p u w e", u=2, e=2)[:, :, pairs, :],
+                    in_=r[b][:].rearrange("p (w u e) -> p u w e", u=2, e=2)[:, :, pairs, :],
+                )
 
             pt = {}
 
@@ -318,7 +341,8 @@ def tile_opposedspindirectringamplitudeupdate_x1_kernel(tc, ta, tb, ba, bb, ga, 
                 if g == 0:
                     pb[b] = psum.tile([128, 4, 128], F32, name="turn", bufs=3)
                 for u in range(2):
-                    nc.tensor.transpose(pb[b][:, 2 * g + u, :], words[:, 256 * g + u : 256 * (g + 1) : 2], ident[:])
+                    first = 256 * u + 128 * g
+                    nc.tensor.transpose(pb[b][:, 2 * g + u, :], words[:, first : first + 128], ident[:])
 
             def p_words(b, g0, g1):
                 half = slice(128 * (b % 2), 128 * (b % 2) + 128)
@@ -380,7 +404,7 @@ def tile_opposedspindirectringamplitudeupdate_x1_kernel(tc, ta, tb, ba, bb, ga, 
                     xa_quantise(i + 1)
                     banks[i + 1, 0] = product(i + 1, 0)
                 else:
-                    narrow(i, 0, 512)
+                    narrow(i, 0, 1)
                 divide(i, 1, banks[i, 1])
                 store_r(i)
                 if i + 1 < BLOCKS:
@@ -393,6 +417,7 @@ def tile_opposedspindirectringamplitudeupdate_x1_kernel(tc, ta, tb, ba, bb, ga, 
                     p_words(i - 1, 0, 2)
                 if i + 3 < BLOCKS:
                     xa_mm(i + 3)
+                busy(1 if i + 3 < BLOCKS else 2)
                 if i + 4 < BLOCKS:
                     root(i + 4)
                 if i + 3 < BLOCKS:
@@ -402,10 +427,10 @@ def tile_opposedspindirectringamplitudeupdate_x1_kernel(tc, ta, tb, ba, bb, ga, 
                 if i + 2 < BLOCKS:
                     xa_add(i + 2)
                 if i < last:
-                    narrow(i, 0, M)
+                    narrow(i, 0, 2)
             turn_p(last, 0)
             p_words(last, 0, 1)
-            narrow(last, 512, M)
+            narrow(last, 1, 2)
             p_quantise(last - 1, 0)
             p_quantise(last - 1, 1)
             store_codes(last - 1, last)

@@ -15,6 +15,7 @@ ACT = mybir.ActivationFunctionType
 N, M, P = 1024, 1024, 512
 FLOPS = 2 * N * N * P + 2 * M * M * P + 2 * N * M * P
 BLOCKS = N // 128
+NS = (2, 5, 6)
 
 
 def tile_opposedspindirectringamplitudeupdate_x1_kernel(tc, ta, tb, ba, bb, ga, gb, delta, out_0, out_1, out_2):
@@ -24,76 +25,83 @@ def tile_opposedspindirectringamplitudeupdate_x1_kernel(tc, ta, tb, ba, bb, ga, 
         pool = ctx.enter_context(tc.tile_pool(name="work", bufs=2))
         psum = ctx.enter_context(tc.psum_pool(name="psum", bufs=2))
 
-        ident = keep.tile([128, 128], F32, name="ident", align_bytes=64)
-
         def keep_tile(shape, dtype, name):
             return keep.tile(shape, dtype, name=name, align_bytes=64)
 
-        graw = {}
-        gf = {}
-        for s in ("a", "b"):
-            graw[s] = keep_tile([128, 2, 4], BF16, "g" + s)
+        ident = keep_tile([128, 128], F32, "ident")
+        graw, gf, raw, btr, gcodes, gscale = {}, {}, {}, {}, {}, {}
+        for s in ("b", "a"):
+            graw[s] = keep_tile([128, 2, 4], BF16, "graw" + s)
             gf[s] = keep_tile([128, 2, 4], F32, "gf" + s)
-        warm = keep.tile([128, 1], F32, name="warm")
-        raw = {}
-        for s in ("a", "b"):
+            btr[s] = keep_tile([128, 1024, 4], BF16, "btr" + s)
             for c in range(2):
                 raw[s, c] = keep_tile([128, 4, P], BF16, "raw%s%d" % (s, c))
+                gcodes[s, c] = keep_tile([128, P], U32, "gcodes%s%d" % (s, c))
+                gscale[s, c] = keep_tile([128, P], U8, "gscale%s%d" % (s, c))
         tbr = [pool.tile([128, 4, M], BF16, name="tbr%d" % c, tag="big", bufs=4, align_bytes=64) for c in range(2)]
         tar = [keep_tile([128, 2, N], BF16, "tar%d" % i) for i in range(4)]
         dr = [keep_tile([128, M], BF16, "dr%d" % b) for b in range(8)]
-        btr = {s: keep_tile([128, 1024, 4], BF16, "btr" + s) for s in ("a", "b")}
-        gcodes = {}
-        gscale = {}
-        for s in ("a", "b"):
-            for c in range(2):
-                gcodes[s, c] = keep_tile([128, 512], U32, "gcodes%s%d" % (s, c))
-                gscale[s, c] = keep_tile([128, 512], U8, "gscale%s%d" % (s, c))
         tbcodes = [keep_tile([128, M], U32, "tbcodes%d" % c) for c in range(2)]
         tbscale = [keep_tile([128, M], U8, "tbscale%d" % c) for c in range(2)]
         xbcodes = keep_tile([128, M], U32, "xbcodes")
         xbscale = keep_tile([128, M], U8, "xbscale")
-        pcodes = [keep_tile([128, 2, 256], U32, "pcodes%d" % q) for q in range(4)]
-        pscale = keep_tile([128, 4, 2, 256], U8, "pscale")
+        pcodes = keep_tile([128, 2, N], U32, "pcodes")
+        pscale = keep_tile([128, 2, N], U8, "pscale")
+        warm = keep.tile([128, 1], F32, name="warm")
+        spare = psum.tile([128, 512], F32, name="spare", bufs=1)
 
         make_identity(nc, ident[:])
         with tc.manual_schedule():
             nc.scalar.dma_start(out=graw["b"][:], in_=gb.rearrange("(c p j) -> p c j", p=128, j=4))
             nc.scalar.dma_start(out=graw["a"][:], in_=ga.rearrange("(c p j) -> p c j", p=128, j=4))
-            for c in range(2):
-                nc.sync.dma_start(out=raw["b", c][:], in_=bb[512 * c : 512 * (c + 1), :].rearrange("(p j) w -> p j w", j=4))
-            for c in range(2):
-                nc.sync.dma_start(out=tbr[c][:], in_=tb[512 * c : 512 * (c + 1), :].rearrange("(p j) w -> p j w", j=4))
-            for c in range(2):
-                nc.sync.dma_start(out=raw["a", c][:], in_=ba[512 * c : 512 * (c + 1), :].rearrange("(p j) w -> p j w", j=4))
-            for i in range(4):
-                nc.sync.dma_start(out=tar[i][:], in_=ta[256 * i : 256 * (i + 1), :].rearrange("(b p) k -> p b k", p=128))
-                nc.sync.dma_start(out=dr[i][:], in_=delta[128 * i : 128 * (i + 1), :])
-            for b in range(4, 8):
+            def load_raw(s, x, c):
+                nc.sync.dma_start(out=raw[s, c][:], in_=x[512 * c : 512 * (c + 1), :].rearrange("(p j) w -> p j w", j=4))
+
+            def load_delta(b):
                 nc.sync.dma_start(out=dr[b][:], in_=delta[128 * b : 128 * (b + 1), :])
 
-            gm = {}
+            def load_ta(q):
+                nc.sync.dma_start(out=tar[q][:], in_=ta[256 * q : 256 * (q + 1), :].rearrange("(b p) k -> p b k", p=128))
 
-            def factor_mult(s, c):
+            load_raw("b", bb, 0)
+            load_raw("b", bb, 1)
+            for c in range(2):
+                nc.sync.dma_start(out=tbr[c][:], in_=tb[512 * c : 512 * (c + 1), :].rearrange("(p j) w -> p j w", j=4))
+            load_delta(0)
+            load_raw("a", ba, 0)
+            load_ta(0)
+            load_raw("a", ba, 1)
+            load_delta(1)
+            load_ta(1)
+            load_delta(2)
+            load_ta(2)
+            load_delta(3)
+            load_ta(3)
+            for b in range(4, 8):
+                load_delta(b)
+
+            gm = {}
+            gi = {}
+
+            def factor_mult(s, c, engine="v"):
                 gm[s, c] = pool.tile([128, 4, P], BF16, name="gm", align_bytes=64)
                 for j in range(4):
-                    nc.vector.tensor_scalar(
-                        out=gm[s, c][:, j, :], in0=raw[s, c][:, j, :], scalar1=gf[s][:, c, j : j + 1], scalar2=None, op0=ALU.mult
-                    )
+                    if engine == "v":
+                        nc.vector.tensor_scalar(
+                            out=gm[s, c][:, j, :], in0=raw[s, c][:, j, :], scalar1=gf[s][:, c, j : j + 1], scalar2=None, op0=ALU.mult
+                        )
+                    else:
+                        nc.scalar.activation(
+                            out=gm[s, c][:, j, :], in_=raw[s, c][:, j, :], func=ACT.Copy, scale=gf[s][:, c, j : j + 1]
+                        )
+
+            def interleave(engine, dst, src):
+                copy = nc.vector.tensor_copy if engine == "v" else nc.scalar.copy
+                copy(out=dst, in_=src.rearrange("p j w -> p w j"))
 
             def factor_copy(s, c):
-                gi = pool.tile([128, 4, 128, 4], BF16, name="gi", align_bytes=64)
-                nc.vector.tensor_copy(out=gi[:], in_=gm[s, c][:].rearrange("p j (m t) -> p t m j", t=4))
-                return gi
-
-            def factor_quantise(s, c, gi):
-                nc.vector.quantize_mx(
-                    out=gcodes[s, c][:].bitcast(FP8X4), scales=gscale[s, c][:], in_=gi[:].rearrange("p t m j -> p (t m j)")
-                )
-
-            tat = {}
-            tac = {}
-            xab = {}
+                gi[s, c] = pool.tile([128, 4, 128, 4], BF16, name="gi", align_bytes=64)
+                nc.vector.tensor_copy(out=gi[s, c][:], in_=gm[s, c][:].rearrange("p j (m t) -> p t m j", t=4))
 
             def turn_b(s, c, h):
                 words = raw[s, c][:].rearrange("p j w -> p (j w)").bitcast(F32)
@@ -106,69 +114,22 @@ def tile_opposedspindirectringamplitudeupdate_x1_kernel(tc, ta, tb, ba, bb, ga, 
                 dst = dst[:, 1024 * c : 1024 * (c + 1)].rearrange("p (q r) -> p q r", r=8)[:, :, 4 * h : 4 * h + 4]
                 nc.scalar.copy(out=dst, in_=bank[:].rearrange("p r q -> p q r"))
 
-            def tb_copy(c, h, engine):
-                ti = pool.tile([128, 512, 4], BF16, name="ti", bufs=4, align_bytes=64)
-                src = tbr[c][:, :, 512 * h : 512 * (h + 1)].rearrange("p j (w i) -> p w j i", i=4)
-                dst = ti[:].rearrange("p (w i) j -> p w j i", i=4)
-                if engine == "v":
-                    nc.vector.tensor_copy(out=dst, in_=src)
-                else:
-                    nc.scalar.copy(out=dst, in_=src)
-                return ti
+            def factor_quantise(s, c):
+                nc.vector.quantize_mx(
+                    out=gcodes[s, c][:].bitcast(FP8X4), scales=gscale[s, c][:], in_=gi[s, c][:].rearrange("p t m j -> p (t m j)")
+                )
 
-            def tb_quantise(c, h, ti):
+            ti = {}
+
+            def tb_copy(c, h, engine):
+                ti[c, h] = pool.tile([128, 512, 4], BF16, name="ti", bufs=4, align_bytes=64)
+                interleave(engine, ti[c, h][:], tbr[c][:, :, 512 * h : 512 * (h + 1)])
+
+            def tb_quantise(c, h):
                 cols = slice(512 * h, 512 * (h + 1))
                 nc.vector.quantize_mx(
-                    out=tbcodes[c][:, cols].bitcast(FP8X4), scales=tbscale[c][:, cols], in_=ti[:].rearrange("p w j -> p (w j)")
+                    out=tbcodes[c][:, cols].bitcast(FP8X4), scales=tbscale[c][:, cols], in_=ti[c, h][:].rearrange("p w j -> p (w j)")
                 )
-
-            def turn_ta(b):
-                words = tar[b // 2][:, b % 2, :].bitcast(F32)
-                bank = psum.tile([128, 4, 128], F32, name="turn", bufs=3)
-                for c in range(2):
-                    for u in range(2):
-                        nc.tensor.transpose(bank[:, 2 * c + u, :], words[:, 256 * c + u : 256 * (c + 1) : 2], ident[:])
-                half = slice(128 * (b % 2), 128 * (b % 2) + 128)
-                if b % 2 == 0:
-                    tat[b // 2] = pool.tile([128, 2, 256, 4], BF16, name="tat", bufs=4, align_bytes=64)
-                nc.scalar.copy(
-                    out=tat[b // 2][:].rearrange("p c n f -> p (c n f)").bitcast(F32).rearrange("p (c n u) -> p c n u", c=2, u=2)[:, :, half, :],
-                    in_=bank[:].rearrange("p (c u) n -> p c n u", c=2),
-                )
-
-            def ta_quantise(q):
-                codes = pool.tile([128, 2, 256], U32, name="tacodes", bufs=4, align_bytes=64)
-                scale = pool.tile([128, 2, 256], U8, name="tascale", bufs=4, align_bytes=64)
-                nc.vector.quantize_mx(
-                    out=codes[:].rearrange("p c n -> p (c n)").bitcast(FP8X4),
-                    scales=scale[:].rearrange("p c n -> p (c n)"),
-                    in_=tat[q][:].rearrange("p c n f -> p (c n f)"),
-                )
-                tac[q] = codes, scale
-
-            def dress_mm(s, moving):
-                bank = psum.tile([128, 4, 128], F32, name="dress", tag="mm", bufs=4)
-                for t in range(4):
-                    cols = slice(128 * t, 128 * (t + 1))
-                    for c in range(2):
-                        codes, scale = moving(c)
-                        nc.tensor.matmul_mx(
-                            out=bank[:, t, :],
-                            lhsT=gcodes[s, c][:, cols].bitcast(FP8X4),
-                            lhsT_scale=gscale[s, c][:, cols],
-                            rhs=codes.bitcast(FP8X4),
-                            rhs_scale=scale,
-                            start=(c == 0),
-                            stop=(c == 1),
-                        )
-                return bank
-
-            def dress_add(s, b, bank, out):
-                nc.vector.tensor_tensor(
-                    out=out, in0=bank[:].rearrange("p t n -> p n t"), in1=btr[s][:, 128 * b : 128 * (b + 1), :], op=ALU.add
-                )
-
-            spare = psum.tile([128, 512], F32, name="spare", bufs=1)
 
             def busy(n):
                 for i in range(n):
@@ -182,14 +143,85 @@ def tile_opposedspindirectringamplitudeupdate_x1_kernel(tc, ta, tb, ba, bb, ga, 
                         stop=True,
                     )
 
-            def xb_mm(b):
-                cols = slice(128 * b, 128 * (b + 1))
-                return dress_mm("b", lambda c: (tbcodes[c][:, cols], tbscale[c][:, cols]))
+            def word_view(tile_ap):
+                return tile_ap.rearrange("p c n f -> p (c n f)").bitcast(F32).rearrange("p (c n u) -> p c n u", c=2, u=2)
 
-            def xa_mm(b):
-                cols = slice(128 * (b % 2), 128 * (b % 2) + 128)
-                codes, scale = tac[b // 2]
-                xab[b] = dress_mm("a", lambda c: (codes[:, c, cols], scale[:, c, cols]))
+            tat, tac = {}, {}
+
+            def turn_ta(b):
+                words = tar[b // 2][:, b % 2, :].bitcast(F32)
+                bank = psum.tile([128, 4, 128], F32, name="turn", bufs=3)
+                for c in range(2):
+                    for u in range(2):
+                        nc.tensor.transpose(bank[:, 2 * c + u, :], words[:, 256 * c + u : 256 * (c + 1) : 2], ident[:])
+                half = slice(128 * (b % 2), 128 * (b % 2) + 128)
+                if b % 2 == 0:
+                    tat[b // 2] = pool.tile([128, 2, 256, 4], BF16, name="tat", bufs=4, align_bytes=64)
+                nc.scalar.copy(out=word_view(tat[b // 2][:])[:, :, half, :], in_=bank[:].rearrange("p (c u) n -> p c n u", c=2))
+
+            def ta_quantise(q):
+                codes = pool.tile([128, 2, 256], U32, name="tacodes", bufs=4, align_bytes=64)
+                scale = pool.tile([128, 2, 256], U8, name="tascale", bufs=4, align_bytes=64)
+                nc.vector.quantize_mx(
+                    out=codes[:].rearrange("p c n -> p (c n)").bitcast(FP8X4),
+                    scales=scale[:].rearrange("p c n -> p (c n)"),
+                    in_=tat[q][:].rearrange("p c n f -> p (c n f)"),
+                )
+                tac[q] = codes, scale
+
+            bank_of = {}
+            xt = {}
+
+            def dress_mm(s, b):
+                bank = psum.tile([128, 4, 128], F32, name="dress", tag="mm", bufs=4)
+                for t in range(4):
+                    cols = slice(128 * t, 128 * (t + 1))
+                    for c in range(2):
+                        if s == "b":
+                            own = slice(128 * b, 128 * (b + 1))
+                            codes, scale = tbcodes[c][:, own], tbscale[c][:, own]
+                        else:
+                            own = slice(128 * (b % 2), 128 * (b % 2) + 128)
+                            codes, scale = tac[b // 2][0][:, c, own], tac[b // 2][1][:, c, own]
+                        nc.tensor.matmul_mx(
+                            out=bank[:, t, :],
+                            lhsT=gcodes[s, c][:, cols].bitcast(FP8X4),
+                            lhsT_scale=gscale[s, c][:, cols],
+                            rhs=codes.bitcast(FP8X4),
+                            rhs_scale=scale,
+                            start=(c == 0),
+                            stop=(c == 1),
+                        )
+                bank_of[s, b] = bank
+
+            def dress_add(s, b):
+                if s == "b":
+                    if b % 4 == 0:
+                        xt[s, b // 4] = pool.tile([128, 512, 4], BF16, name="xtb", bufs=2, align_bytes=64)
+                    out = xt[s, b // 4][:, 128 * (b % 4) : 128 * (b % 4) + 128, :]
+                else:
+                    xt[s, b] = pool.tile([128, 128, 4], BF16, name="xta", bufs=3, align_bytes=64)
+                    out = xt[s, b][:]
+                nc.vector.tensor_tensor(
+                    out=out,
+                    in0=bank_of[s, b][:].rearrange("p t n -> p n t"),
+                    in1=btr[s][:, 128 * b : 128 * (b + 1), :],
+                    op=ALU.add,
+                )
+
+            def xb_quantise(h):
+                cols = slice(512 * h, 512 * (h + 1))
+                nc.vector.quantize_mx(
+                    out=xbcodes[:, cols].bitcast(FP8X4), scales=xbscale[:, cols], in_=xt["b", h][:].rearrange("p n f -> p (n f)")
+                )
+
+            xac = {}
+
+            def xa_quantise(b):
+                codes = pool.tile([128, 128], U32, name="xacodes", bufs=3, align_bytes=64)
+                scale = pool.tile([128, 128], U8, name="xascale", bufs=3, align_bytes=64)
+                nc.vector.quantize_mx(out=codes[:].bitcast(FP8X4), scales=scale[:], in_=xt["a", b][:].rearrange("p n f -> p (n f)"))
+                xac[b] = codes, scale
 
             recs = {}
 
@@ -202,105 +234,7 @@ def tile_opposedspindirectringamplitudeupdate_x1_kernel(tc, ta, tb, ba, bb, ga, 
                 rec = recs[b // 2][:, b % 2, :]
                 nc.scalar.activation(out=rec, in_=rec, func=ACT.Square)
 
-            nc.vector.memset(warm[:], 1.0)
-            nc.scalar.activation(out=warm[:], in_=warm[:], func=ACT.Abs_reciprocal_sqrt)
-            for s in ("b", "a"):
-                nc.vector.tensor_copy(out=gf[s][:], in_=graw[s][:])
-            factor_mult("b", 0)
-            gi = [factor_copy("b", 0)]
-            factor_mult("b", 1)
-            gi.append(factor_copy("b", 1))
-            for c in range(2):
-                for h in range(2):
-                    turn_b("b", c, h)
-            ti = {}
-            factor_quantise("b", 0, gi[0])
-            ti[0, 0] = tb_copy(0, 0, "v")
-            ti[0, 1] = tb_copy(0, 1, "s")
-            busy(4)
-            factor_quantise("b", 1, gi[1])
-            tb_quantise(0, 0, ti[0, 0])
-            ti[1, 0] = tb_copy(1, 0, "s")
-            ti[1, 1] = tb_copy(1, 1, "s")
-            factor_mult("a", 0)
-            tb_quantise(0, 1, ti[0, 1])
-            tb_quantise(1, 0, ti[1, 0])
-            gi = [factor_copy("a", 0)]
-            turn_b("a", 0, 0)
-            turn_b("a", 0, 1)
-            busy(2)
-            root(0)
-            xbt = {}
-            xbb = {}
-
-            def xb_add(b):
-                if b % 4 == 0:
-                    xbt[b // 4] = pool.tile([128, 512, 4], BF16, name="xbt", bufs=2, align_bytes=64)
-                dress_add("b", b, xbb[b], xbt[b // 4][:, 128 * (b % 4) : 128 * (b % 4) + 128, :])
-
-            def xb_quantise(q):
-                cols = slice(512 * q, 512 * (q + 1))
-                nc.vector.quantize_mx(
-                    out=xbcodes[:, cols].bitcast(FP8X4), scales=xbscale[:, cols], in_=xbt[q][:].rearrange("p n f -> p (n f)")
-                )
-
-            for b in range(4):
-                xbb[b] = xb_mm(b)
-            xb_add(0)
-            xb_add(1)
-            turn_b("a", 1, 0)
-            factor_mult("a", 1)
-            turn_b("a", 1, 1)
-            root(1)
-            xb_add(2)
-            xb_add(3)
-            gi.append(factor_copy("a", 1))
-            turn_ta(0)
-            turn_ta(1)
-            busy(1)
-            tb_quantise(1, 1, ti[1, 1])
-            for b in range(4, 8):
-                xbb[b] = xb_mm(b)
-            xb_quantise(0)
-            square(0)
-            turn_ta(2)
-            turn_ta(3)
-            busy(1)
-            factor_quantise("a", 0, gi[0])
-            xb_add(4)
-            square(1)
-            xb_add(5)
-            factor_quantise("a", 1, gi[1])
-            ta_quantise(0)
-            xb_add(6)
-            turn_ta(4)
-            turn_ta(5)
-            busy(1)
-            root(2)
-            xb_add(7)
-            xa_mm(0)
-            xa_mm(1)
-            root(3)
-            square(2)
-            ta_quantise(1)
-            xb_quantise(1)
-
-            xa = {}
-            xac = {}
-
-            def xa_add(b):
-                bank = xab[b]
-                xa[b] = pool.tile([128, 128, 4], BF16, name="xa", bufs=3, align_bytes=64)
-                dress_add("a", b, bank, xa[b][:])
-
-            def xa_quantise(b):
-                codes = pool.tile([128, 128], U32, name="xacodes", bufs=3, align_bytes=64)
-                scale = pool.tile([128, 128], U8, name="xascale", bufs=3, align_bytes=64)
-                nc.vector.quantize_mx(out=codes[:].bitcast(FP8X4), scales=scale[:], in_=xa[b][:].rearrange("p n f -> p (n f)"))
-                xac[b] = codes, scale
-
-            r = {}
-            rb = {}
+            prod = {}
 
             def product(b, h):
                 cols = slice(512 * h, 512 * (h + 1))
@@ -314,27 +248,28 @@ def tile_opposedspindirectringamplitudeupdate_x1_kernel(tc, ta, tb, ba, bb, ga, 
                     start=True,
                     stop=True,
                 )
-                return bank
+                prod[b, h] = bank
 
-            def divide(b, h, bank):
+            r, rb = {}, {}
+
+            def divide(b, h):
                 cols = slice(512 * h, 512 * (h + 1))
                 if h == 0:
-                    r[b] = pool.tile([128, M], F32, name="r", bufs=4)
-                    rb[b] = pool.tile([128, M], BF16, name="rb", bufs=3)
+                    r[b] = pool.tile([128, M], F32, name="r", bufs=3)
+                    rb[b] = pool.tile([128, M], BF16, name="rb", bufs=2)
                 nc.vector.scalar_tensor_tensor(
-                    out=r[b][:, cols], in0=bank[:], scalar=-1.0, in1=recs[b // 2][:, b % 2, cols], op0=ALU.mult, op1=ALU.mult
+                    out=r[b][:, cols], in0=prod[b, h][:], scalar=-1.0, in1=recs[b // 2][:, b % 2, cols], op0=ALU.mult, op1=ALU.mult
                 )
 
-            def narrow(b, g0, g1):
+            def narrow(b, g0, g1, engine="v"):
                 pairs = slice(128 * g0, 128 * g1)
-                nc.vector.tensor_copy(
+                copy = nc.vector.tensor_copy if engine == "v" else nc.scalar.copy
+                copy(
                     out=rb[b][:].rearrange("p (u w e) -> p u w e", u=2, e=2)[:, :, pairs, :],
                     in_=r[b][:].rearrange("p (w u e) -> p u w e", u=2, e=2)[:, :, pairs, :],
                 )
 
-            pt = {}
-
-            pb = {}
+            pb, pt = {}, {}
 
             def turn_p(b, g):
                 words = rb[b][:].bitcast(F32)
@@ -349,94 +284,158 @@ def tile_opposedspindirectringamplitudeupdate_x1_kernel(tc, ta, tb, ba, bb, ga, 
                 if b % 2 == 0 and g0 == 0:
                     pt[b // 2] = pool.tile([128, 2, 256, 4], BF16, name="pt", bufs=2, align_bytes=64)
                 nc.scalar.copy(
-                    out=pt[b // 2][:].rearrange("p c n f -> p (c n f)").bitcast(F32).rearrange("p (c n u) -> p c n u", c=2, u=2)[:, g0:g1, half, :],
+                    out=word_view(pt[b // 2][:])[:, g0:g1, half, :],
                     in_=pb[b][:, 2 * g0 : 2 * g1, :].rearrange("p (c u) n -> p c n u", u=2),
                 )
 
-            def p_quantise_pair(q):
+            def p_quantise(b0, b1, g):
+                cols = slice(128 * b0, 128 * b1)
+                own = slice(128 * (b0 % 2), 128 * (b0 % 2) + 128 * (b1 - b0))
                 nc.vector.quantize_mx(
-                    out=pcodes[q][:].rearrange("p g n -> p (g n)").bitcast(FP8X4),
-                    scales=pscale[:, q, :, :].rearrange("p g n -> p (g n)"),
-                    in_=pt[q][:].rearrange("p g n f -> p (g n f)"),
+                    out=pcodes[:, g, cols].bitcast(FP8X4),
+                    scales=pscale[:, g, cols],
+                    in_=pt[b0 // 2][:, g, own, :].rearrange("p n f -> p (n f)"),
                 )
 
-            def p_quantise(b, g):
-                half = slice(128 * (b % 2), 128 * (b % 2) + 128)
-                nc.vector.quantize_mx(
-                    out=pcodes[b // 2][:, g, half].bitcast(FP8X4),
-                    scales=pscale[:, b // 2, g, half],
-                    in_=pt[b // 2][:, g, half, :].rearrange("p n f -> p (n f)"),
-                )
-
-            def store_r(b):
-                nc.sync.dma_start(out=out_0[128 * b : 128 * (b + 1), :], in_=r[b][:])
+            def store_r(b, c0, c1):
+                nc.sync.dma_start(out=out_0[128 * b : 128 * (b + 1), c0:c1], in_=r[b][:, c0:c1])
 
             def store_codes(b0, b1):
-                n = 128 * (b1 - b0)
-                n0 = 128 * (b0 % 2)
+                cols = slice(128 * b0, 128 * b1)
                 nc.sync.dma_start(
-                    out=out_1[:, :, 128 * b0 : 128 * b1, :].rearrange("g p n f -> p g (n f)").bitcast(I32),
-                    in_=pcodes[b0 // 2][:, :, n0 : n0 + n].bitcast(I32),
+                    out=out_1[:, :, cols, :].rearrange("g p n f -> p g (n f)").bitcast(I32), in_=pcodes[:, :, cols].bitcast(I32)
                 )
 
-            def store_scales(q, queues):
+            def store_scales(b0, b1, queues):
+                cols = slice(128 * b0, 128 * b1)
                 for quad in range(4):
                     queues[quad % 2].dma_start(
-                        out=out_2[:, 4 * quad : 4 * quad + 4, 256 * q : 256 * (q + 1)].rearrange("g r n -> r g n").bitcast(I32),
-                        in_=pscale[32 * quad : 32 * quad + 4, q, :, :].bitcast(I32),
+                        out=out_2[:, 4 * quad : 4 * quad + 4, cols].rearrange("g r n -> r g n").bitcast(I32),
+                        in_=pscale[32 * quad : 32 * quad + 4, :, cols].bitcast(I32),
                     )
 
-            xa_add(0)
-            xa_add(1)
-            xa_mm(2)
+            def p_pair(q):
+                p_quantise(2 * q, 2 * q + 2, 0)
+                p_quantise(2 * q, 2 * q + 2, 1)
+                store_codes(2 * q, 2 * q + 2)
+                if q == 2:
+                    store_scales(0, 6, (nc.sync, nc.sync))
+
+
+            nc.vector.memset(warm[:], 1.0)
+            nc.scalar.activation(out=warm[:], in_=warm[:], func=ACT.Abs_reciprocal_sqrt)
+            nc.vector.tensor_copy(out=gf["b"][:], in_=graw["b"][:])
+            turn_b("b", 0, 0)
+            turn_b("b", 0, 1)
+            turn_b("b", 1, 0)
+            turn_b("b", 1, 1)
+            factor_mult("b", 0)
+            factor_mult("b", 1)
+            factor_copy("b", 0)
+            tb_copy(0, 1, "s")
+            tb_copy(1, 0, "s")
+            factor_quantise("b", 0)
+            busy(3)
+            tb_copy(0, 0, "v")
+            tb_copy(1, 1, "s")
+            factor_copy("b", 1)
+            nc.vector.tensor_copy(out=gf["a"][:], in_=graw["a"][:])
+            turn_b("a", 0, 1)
+            tb_quantise(0, 0)
+            factor_quantise("b", 1)
+            factor_mult("a", 0)
+            busy(1)
+            turn_ta(0)
+            turn_ta(1)
+            tb_quantise(0, 1)
+            root(0)
+            tb_quantise(1, 0)
+            for b in range(4): dress_mm("b", b)
+            factor_copy("a", 0)
+            factor_mult("a", 1)
+            factor_quantise("a", 0)
+            turn_b("a", 0, 0)
+            root(1)
+            dress_add("b", 0)
+            dress_add("b", 1)
+            factor_copy("a", 1)
+            square(0)
+            tb_quantise(1, 1)
+            factor_quantise("a", 1)
+            ta_quantise(0)
+            turn_b("a", 1, 1)
+            turn_ta(2)
+            turn_ta(3)
+            root(2)
+            root(3)
+            dress_mm("b", 4)
+            dress_mm("b", 5)
+            dress_add("b", 2)
+            dress_add("b", 3)
+            square(2)
+            dress_mm("a", 0)
+            dress_add("b", 4)
+            dress_mm("b", 6)
+            dress_mm("b", 7)
+            xb_quantise(0)
+            turn_ta(4)
+            turn_b("a", 1, 0)
+            dress_add("a", 0)
+            dress_add("b", 5)
+            dress_add("b", 6)
+            turn_ta(5)
+            dress_add("b", 7)
+            dress_mm("a", 1)
             xa_quantise(0)
-            banks = {}
-            for h in range(2):
-                banks[0, h] = product(0, h)
+            xb_quantise(1)
+            ta_quantise(1)
+            dress_add("a", 1)
+            product(0, 0)
+            product(0, 1)
+            dress_mm("a", 2)
+            busy(1)
+            square(1)
             last = BLOCKS - 1
             for i in range(BLOCKS):
-                divide(i, 0, banks[i, 0])
-                if i >= 3 and i % 2 == 1:
-                    p_quantise_pair(i // 2 - 1)
-                    store_codes(i - 3, i - 1)
-                    store_scales(i // 2 - 1, (nc.sync, nc.sync))
-                if i + 1 < BLOCKS:
-                    xa_quantise(i + 1)
-                    banks[i + 1, 0] = product(i + 1, 0)
-                else:
-                    narrow(i, 0, 1)
-                divide(i, 1, banks[i, 1])
-                store_r(i)
-                if i + 1 < BLOCKS:
-                    banks[i + 1, 1] = product(i + 1, 1)
+                if i < 4:
+                    root(i + 4)
+                divide(i, 0)
                 if i < 2:
                     turn_ta(i + 6)
+                if i < last:
+                    xa_quantise(i + 1)
+                if i in (3, 5, 7):
+                    p_pair(i // 2 - 1)
                 if i >= 1:
                     turn_p(i - 1, 0)
+                if i >= 1:
                     turn_p(i - 1, 1)
+                if i < last:
+                    product(i + 1, 0)
+                divide(i, 1)
+                if i >= 1:
                     p_words(i - 1, 0, 2)
-                if i + 3 < BLOCKS:
-                    xa_mm(i + 3)
-                busy(1 if i + 3 < BLOCKS else 2)
-                if i + 4 < BLOCKS:
-                    root(i + 4)
-                if i + 3 < BLOCKS:
+                if i < 6:
+                    dress_add("a", i + 2)
+                store_r(i, 0, M)
+                if i < last:
+                    product(i + 1, 1)
+                if i < 5:
+                    dress_mm("a", i + 3)
+                narrow(i, 0, 2, "s" if i in NS else "v")
+                if i < 5:
                     square(i + 3)
+                busy(1 if i < 5 else 2)
                 if i in (0, 2):
                     ta_quantise(2 + i // 2)
-                if i + 2 < BLOCKS:
-                    xa_add(i + 2)
-                if i < last:
-                    narrow(i, 0, 2)
+            p_quantise(6, 7, 0)
+            p_quantise(6, 7, 1)
+            store_codes(6, 7)
             turn_p(last, 0)
-            p_words(last, 0, 1)
-            narrow(last, 1, 2)
-            p_quantise(last - 1, 0)
-            p_quantise(last - 1, 1)
-            store_codes(last - 1, last)
             turn_p(last, 1)
+            p_words(last, 0, 1)
+            p_quantise(7, 8, 0)
             p_words(last, 1, 2)
-            p_quantise(last, 0)
-            p_quantise(last, 1)
-            store_codes(last, BLOCKS)
-            store_scales(3, (nc.sync, nc.scalar))
+            p_quantise(7, 8, 1)
+            store_codes(7, 8)
+            store_scales(6, 8, (nc.sync, nc.scalar))

from contextlib import ExitStack

import concourse.mybir as mybir
from concourse.masks import make_identity

F32 = mybir.dt.float32
BF16 = mybir.dt.bfloat16
I32 = mybir.dt.int32
U32 = mybir.dt.uint32
U8 = mybir.dt.uint8
FP8X4 = mybir.dt.float8_e4m3fn_x4
ALU = mybir.AluOpType
ACT = mybir.ActivationFunctionType

N, M, P = 1024, 1024, 512
FLOPS = 2 * N * N * P + 2 * M * M * P + 2 * N * M * P
BLOCKS = N // 128
NS = (2, 5, 6)


def tile_opposedspindirectringamplitudeupdate_x1_kernel(tc, ta, tb, ba, bb, ga, gb, delta, out_0, out_1, out_2):
    nc = tc.nc
    with ExitStack() as ctx:
        keep = ctx.enter_context(tc.tile_pool(name="keep", bufs=1))
        pool = ctx.enter_context(tc.tile_pool(name="work", bufs=2))
        psum = ctx.enter_context(tc.psum_pool(name="psum", bufs=2))

        def keep_tile(shape, dtype, name):
            return keep.tile(shape, dtype, name=name, align_bytes=64)

        ident = keep_tile([128, 128], F32, "ident")
        graw, gf, raw, btr, gcodes, gscale = {}, {}, {}, {}, {}, {}
        for s in ("b", "a"):
            graw[s] = keep_tile([128, 2, 4], BF16, "graw" + s)
            gf[s] = keep_tile([128, 2, 4], F32, "gf" + s)
            btr[s] = keep_tile([128, 1024, 4], BF16, "btr" + s)
            for c in range(2):
                raw[s, c] = keep_tile([128, 4, P], BF16, "raw%s%d" % (s, c))
                gcodes[s, c] = keep_tile([128, P], U32, "gcodes%s%d" % (s, c))
                gscale[s, c] = keep_tile([128, P], U8, "gscale%s%d" % (s, c))
        tbr = [pool.tile([128, 4, M], BF16, name="tbr%d" % c, tag="big", bufs=4, align_bytes=64) for c in range(2)]
        tar = [keep_tile([128, 2, N], BF16, "tar%d" % i) for i in range(4)]
        dr = [keep_tile([128, M], BF16, "dr%d" % b) for b in range(8)]
        tbcodes = [keep_tile([128, M], U32, "tbcodes%d" % c) for c in range(2)]
        tbscale = [keep_tile([128, M], U8, "tbscale%d" % c) for c in range(2)]
        xbcodes = keep_tile([128, M], U32, "xbcodes")
        xbscale = keep_tile([128, M], U8, "xbscale")
        pcodes = keep_tile([128, 2, N], U32, "pcodes")
        pscale = keep_tile([128, 2, N], U8, "pscale")
        warm = keep.tile([128, 1], F32, name="warm")
        spare = psum.tile([128, 512], F32, name="spare", bufs=1)

        make_identity(nc, ident[:])
        with tc.manual_schedule():
            nc.scalar.dma_start(out=graw["b"][:], in_=gb.rearrange("(c p j) -> p c j", p=128, j=4))
            nc.scalar.dma_start(out=graw["a"][:], in_=ga.rearrange("(c p j) -> p c j", p=128, j=4))
            def load_raw(s, x, c):
                nc.sync.dma_start(out=raw[s, c][:], in_=x[512 * c : 512 * (c + 1), :].rearrange("(p j) w -> p j w", j=4))

            def load_delta(b):
                nc.sync.dma_start(out=dr[b][:], in_=delta[128 * b : 128 * (b + 1), :])

            def load_ta(q):
                nc.sync.dma_start(out=tar[q][:], in_=ta[256 * q : 256 * (q + 1), :].rearrange("(b p) k -> p b k", p=128))

            load_raw("b", bb, 0)
            load_raw("b", bb, 1)
            for c in range(2):
                nc.sync.dma_start(out=tbr[c][:], in_=tb[512 * c : 512 * (c + 1), :].rearrange("(p j) w -> p j w", j=4))
            load_delta(0)
            load_raw("a", ba, 0)
            load_ta(0)
            load_raw("a", ba, 1)
            load_delta(1)
            load_ta(1)
            load_delta(2)
            load_ta(2)
            load_delta(3)
            load_ta(3)
            for b in range(4, 8):
                load_delta(b)

            gm = {}
            gi = {}

            def factor_mult(s, c, engine="v"):
                gm[s, c] = pool.tile([128, 4, P], BF16, name="gm", align_bytes=64)
                for j in range(4):
                    if engine == "v":
                        nc.vector.tensor_scalar(
                            out=gm[s, c][:, j, :], in0=raw[s, c][:, j, :], scalar1=gf[s][:, c, j : j + 1], scalar2=None, op0=ALU.mult
                        )
                    else:
                        nc.scalar.activation(
                            out=gm[s, c][:, j, :], in_=raw[s, c][:, j, :], func=ACT.Copy, scale=gf[s][:, c, j : j + 1]
                        )

            def interleave(engine, dst, src):
                copy = nc.vector.tensor_copy if engine == "v" else nc.scalar.copy
                copy(out=dst, in_=src.rearrange("p j w -> p w j"))

            def factor_copy(s, c):
                gi[s, c] = pool.tile([128, 4, 128, 4], BF16, name="gi", align_bytes=64)
                nc.vector.tensor_copy(out=gi[s, c][:], in_=gm[s, c][:].rearrange("p j (m t) -> p t m j", t=4))

            def turn_b(s, c, h):
                words = raw[s, c][:].rearrange("p j w -> p (j w)").bitcast(F32)
                bank = psum.tile([128, 4, 128], F32, name="turn", bufs=3)
                for jj in range(2):
                    for u in range(2):
                        j = 2 * h + jj
                        nc.tensor.transpose(bank[:, 2 * jj + u, :], words[:, 256 * j + u : 256 * (j + 1) : 2], ident[:])
                dst = btr[s][:].rearrange("p n f -> p (n f)").bitcast(F32)
                dst = dst[:, 1024 * c : 1024 * (c + 1)].rearrange("p (q r) -> p q r", r=8)[:, :, 4 * h : 4 * h + 4]
                nc.scalar.copy(out=dst, in_=bank[:].rearrange("p r q -> p q r"))

            def factor_quantise(s, c):
                nc.vector.quantize_mx(
                    out=gcodes[s, c][:].bitcast(FP8X4), scales=gscale[s, c][:], in_=gi[s, c][:].rearrange("p t m j -> p (t m j)")
                )

            ti = {}

            def tb_copy(c, h, engine):
                ti[c, h] = pool.tile([128, 512, 4], BF16, name="ti", bufs=4, align_bytes=64)
                interleave(engine, ti[c, h][:], tbr[c][:, :, 512 * h : 512 * (h + 1)])

            def tb_quantise(c, h):
                cols = slice(512 * h, 512 * (h + 1))
                nc.vector.quantize_mx(
                    out=tbcodes[c][:, cols].bitcast(FP8X4), scales=tbscale[c][:, cols], in_=ti[c, h][:].rearrange("p w j -> p (w j)")
                )

            def busy(n):
                for i in range(n):
                    nc.tensor.matmul_mx(
                        out=spare[:],
                        lhsT=gcodes["b", 0][:, 0:128].bitcast(FP8X4),
                        lhsT_scale=gscale["b", 0][:, 0:128],
                        rhs=gcodes["b", 0][:].bitcast(FP8X4),
                        rhs_scale=gscale["b", 0][:],
                        start=True,
                        stop=True,
                    )

            def word_view(tile_ap):
                return tile_ap.rearrange("p c n f -> p (c n f)").bitcast(F32).rearrange("p (c n u) -> p c n u", c=2, u=2)

            tat, tac = {}, {}

            def turn_ta(b):
                words = tar[b // 2][:, b % 2, :].bitcast(F32)
                bank = psum.tile([128, 4, 128], F32, name="turn", bufs=3)
                for c in range(2):
                    for u in range(2):
                        nc.tensor.transpose(bank[:, 2 * c + u, :], words[:, 256 * c + u : 256 * (c + 1) : 2], ident[:])
                half = slice(128 * (b % 2), 128 * (b % 2) + 128)
                if b % 2 == 0:
                    tat[b // 2] = pool.tile([128, 2, 256, 4], BF16, name="tat", bufs=4, align_bytes=64)
                nc.scalar.copy(out=word_view(tat[b // 2][:])[:, :, half, :], in_=bank[:].rearrange("p (c u) n -> p c n u", c=2))

            def ta_quantise(q):
                codes = pool.tile([128, 2, 256], U32, name="tacodes", bufs=4, align_bytes=64)
                scale = pool.tile([128, 2, 256], U8, name="tascale", bufs=4, align_bytes=64)
                nc.vector.quantize_mx(
                    out=codes[:].rearrange("p c n -> p (c n)").bitcast(FP8X4),
                    scales=scale[:].rearrange("p c n -> p (c n)"),
                    in_=tat[q][:].rearrange("p c n f -> p (c n f)"),
                )
                tac[q] = codes, scale

            bank_of = {}
            xt = {}

            def dress_mm(s, b):
                bank = psum.tile([128, 4, 128], F32, name="dress", tag="mm", bufs=4)
                for t in range(4):
                    cols = slice(128 * t, 128 * (t + 1))
                    for c in range(2):
                        if s == "b":
                            own = slice(128 * b, 128 * (b + 1))
                            codes, scale = tbcodes[c][:, own], tbscale[c][:, own]
                        else:
                            own = slice(128 * (b % 2), 128 * (b % 2) + 128)
                            codes, scale = tac[b // 2][0][:, c, own], tac[b // 2][1][:, c, own]
                        nc.tensor.matmul_mx(
                            out=bank[:, t, :],
                            lhsT=gcodes[s, c][:, cols].bitcast(FP8X4),
                            lhsT_scale=gscale[s, c][:, cols],
                            rhs=codes.bitcast(FP8X4),
                            rhs_scale=scale,
                            start=(c == 0),
                            stop=(c == 1),
                        )
                bank_of[s, b] = bank

            def dress_add(s, b):
                if s == "b":
                    if b % 4 == 0:
                        xt[s, b // 4] = pool.tile([128, 512, 4], BF16, name="xtb", bufs=2, align_bytes=64)
                    out = xt[s, b // 4][:, 128 * (b % 4) : 128 * (b % 4) + 128, :]
                else:
                    xt[s, b] = pool.tile([128, 128, 4], BF16, name="xta", bufs=3, align_bytes=64)
                    out = xt[s, b][:]
                nc.vector.tensor_tensor(
                    out=out,
                    in0=bank_of[s, b][:].rearrange("p t n -> p n t"),
                    in1=btr[s][:, 128 * b : 128 * (b + 1), :],
                    op=ALU.add,
                )

            def xb_quantise(h):
                cols = slice(512 * h, 512 * (h + 1))
                nc.vector.quantize_mx(
                    out=xbcodes[:, cols].bitcast(FP8X4), scales=xbscale[:, cols], in_=xt["b", h][:].rearrange("p n f -> p (n f)")
                )

            xac = {}

            def xa_quantise(b):
                codes = pool.tile([128, 128], U32, name="xacodes", bufs=3, align_bytes=64)
                scale = pool.tile([128, 128], U8, name="xascale", bufs=3, align_bytes=64)
                nc.vector.quantize_mx(out=codes[:].bitcast(FP8X4), scales=scale[:], in_=xt["a", b][:].rearrange("p n f -> p (n f)"))
                xac[b] = codes, scale

            recs = {}

            def root(b):
                if b % 2 == 0:
                    recs[b // 2] = pool.tile([128, 2, M], F32, name="recs", tag="big", bufs=4, align_bytes=64)
                nc.scalar.activation(out=recs[b // 2][:, b % 2, :], in_=dr[b][:], func=ACT.Abs_reciprocal_sqrt)

            def square(b):
                rec = recs[b // 2][:, b % 2, :]
                nc.scalar.activation(out=rec, in_=rec, func=ACT.Square)

            prod = {}

            def product(b, h):
                cols = slice(512 * h, 512 * (h + 1))
                bank = psum.tile([128, 512], F32, name="prod", tag="mm", bufs=4)
                nc.tensor.matmul_mx(
                    out=bank[:],
                    lhsT=xac[b][0][:].bitcast(FP8X4),
                    lhsT_scale=xac[b][1][:],
                    rhs=xbcodes[:, cols].bitcast(FP8X4),
                    rhs_scale=xbscale[:, cols],
                    start=True,
                    stop=True,
                )
                prod[b, h] = bank

            r, rb = {}, {}

            def divide(b, h):
                cols = slice(512 * h, 512 * (h + 1))
                if h == 0:
                    r[b] = pool.tile([128, M], F32, name="r", bufs=3)
                    rb[b] = pool.tile([128, M], BF16, name="rb", bufs=2)
                nc.vector.scalar_tensor_tensor(
                    out=r[b][:, cols], in0=prod[b, h][:], scalar=-1.0, in1=recs[b // 2][:, b % 2, cols], op0=ALU.mult, op1=ALU.mult
                )

            def narrow(b, g0, g1, engine="v"):
                pairs = slice(128 * g0, 128 * g1)
                copy = nc.vector.tensor_copy if engine == "v" else nc.scalar.copy
                copy(
                    out=rb[b][:].rearrange("p (u w e) -> p u w e", u=2, e=2)[:, :, pairs, :],
                    in_=r[b][:].rearrange("p (w u e) -> p u w e", u=2, e=2)[:, :, pairs, :],
                )

            pb, pt = {}, {}

            def turn_p(b, g):
                words = rb[b][:].bitcast(F32)
                if g == 0:
                    pb[b] = psum.tile([128, 4, 128], F32, name="turn", bufs=3)
                for u in range(2):
                    first = 256 * u + 128 * g
                    nc.tensor.transpose(pb[b][:, 2 * g + u, :], words[:, first : first + 128], ident[:])

            def p_words(b, g0, g1):
                half = slice(128 * (b % 2), 128 * (b % 2) + 128)
                if b % 2 == 0 and g0 == 0:
                    pt[b // 2] = pool.tile([128, 2, 256, 4], BF16, name="pt", bufs=2, align_bytes=64)
                nc.scalar.copy(
                    out=word_view(pt[b // 2][:])[:, g0:g1, half, :],
                    in_=pb[b][:, 2 * g0 : 2 * g1, :].rearrange("p (c u) n -> p c n u", u=2),
                )

            def p_quantise(b0, b1, g):
                cols = slice(128 * b0, 128 * b1)
                own = slice(128 * (b0 % 2), 128 * (b0 % 2) + 128 * (b1 - b0))
                nc.vector.quantize_mx(
                    out=pcodes[:, g, cols].bitcast(FP8X4),
                    scales=pscale[:, g, cols],
                    in_=pt[b0 // 2][:, g, own, :].rearrange("p n f -> p (n f)"),
                )

            def store_r(b, c0, c1):
                nc.sync.dma_start(out=out_0[128 * b : 128 * (b + 1), c0:c1], in_=r[b][:, c0:c1])

            def store_codes(b0, b1):
                cols = slice(128 * b0, 128 * b1)
                nc.sync.dma_start(
                    out=out_1[:, :, cols, :].rearrange("g p n f -> p g (n f)").bitcast(I32), in_=pcodes[:, :, cols].bitcast(I32)
                )

            def store_scales(b0, b1, queues):
                cols = slice(128 * b0, 128 * b1)
                for quad in range(4):
                    queues[quad % 2].dma_start(
                        out=out_2[:, 4 * quad : 4 * quad + 4, cols].rearrange("g r n -> r g n").bitcast(I32),
                        in_=pscale[32 * quad : 32 * quad + 4, :, cols].bitcast(I32),
                    )

            def p_pair(q):
                p_quantise(2 * q, 2 * q + 2, 0)
                p_quantise(2 * q, 2 * q + 2, 1)
                store_codes(2 * q, 2 * q + 2)
                if q == 2:
                    store_scales(0, 6, (nc.sync, nc.sync))


            nc.vector.memset(warm[:], 1.0)
            nc.scalar.activation(out=warm[:], in_=warm[:], func=ACT.Abs_reciprocal_sqrt)
            nc.vector.tensor_copy(out=gf["b"][:], in_=graw["b"][:])
            turn_b("b", 0, 0)
            turn_b("b", 0, 1)
            turn_b("b", 1, 0)
            turn_b("b", 1, 1)
            factor_mult("b", 0)
            factor_mult("b", 1)
            factor_copy("b", 0)
            tb_copy(0, 1, "s")
            tb_copy(1, 0, "s")
            factor_quantise("b", 0)
            busy(3)
            tb_copy(0, 0, "v")
            tb_copy(1, 1, "s")
            factor_copy("b", 1)
            nc.vector.tensor_copy(out=gf["a"][:], in_=graw["a"][:])
            turn_b("a", 0, 1)
            tb_quantise(0, 0)
            factor_quantise("b", 1)
            factor_mult("a", 0)
            busy(1)
            turn_ta(0)
            turn_ta(1)
            tb_quantise(0, 1)
            root(0)
            tb_quantise(1, 0)
            for b in range(4): dress_mm("b", b)
            factor_copy("a", 0)
            factor_mult("a", 1)
            factor_quantise("a", 0)
            turn_b("a", 0, 0)
            root(1)
            dress_add("b", 0)
            dress_add("b", 1)
            factor_copy("a", 1)
            square(0)
            tb_quantise(1, 1)
            factor_quantise("a", 1)
            ta_quantise(0)
            turn_b("a", 1, 1)
            turn_ta(2)
            turn_ta(3)
            root(2)
            root(3)
            dress_mm("b", 4)
            dress_mm("b", 5)
            dress_add("b", 2)
            dress_add("b", 3)
            square(2)
            dress_mm("a", 0)
            dress_add("b", 4)
            dress_mm("b", 6)
            dress_mm("b", 7)
            xb_quantise(0)
            turn_ta(4)
            turn_b("a", 1, 0)
            dress_add("a", 0)
            dress_add("b", 5)
            dress_add("b", 6)
            turn_ta(5)
            dress_add("b", 7)
            dress_mm("a", 1)
            xa_quantise(0)
            xb_quantise(1)
            ta_quantise(1)
            dress_add("a", 1)
            product(0, 0)
            product(0, 1)
            dress_mm("a", 2)
            busy(1)
            square(1)
            last = BLOCKS - 1
            for i in range(BLOCKS):
                if i < 4:
                    root(i + 4)
                divide(i, 0)
                if i < 2:
                    turn_ta(i + 6)
                if i < last:
                    xa_quantise(i + 1)
                if i in (3, 5, 7):
                    p_pair(i // 2 - 1)
                if i >= 1:
                    turn_p(i - 1, 0)
                if i >= 1:
                    turn_p(i - 1, 1)
                if i < last:
                    product(i + 1, 0)
                divide(i, 1)
                if i >= 1:
                    p_words(i - 1, 0, 2)
                if i < 6:
                    dress_add("a", i + 2)
                store_r(i, 0, M)
                if i < last:
                    product(i + 1, 1)
                if i < 5:
                    dress_mm("a", i + 3)
                narrow(i, 0, 2, "s" if i in NS else "v")
                if i < 5:
                    square(i + 3)
                busy(1 if i < 5 else 2)
                if i in (0, 2):
                    ta_quantise(2 + i // 2)
            p_quantise(6, 7, 0)
            p_quantise(6, 7, 1)
            store_codes(6, 7)
            turn_p(last, 0)
            turn_p(last, 1)
            p_words(last, 0, 1)
            p_quantise(7, 8, 0)
            p_words(last, 1, 2)
            p_quantise(7, 8, 1)
            store_codes(7, 8)
            store_scales(6, 8, (nc.sync, nc.scalar))
